import numpy as np
import ml_dtypes


def mxq(x, axis, fmt="e4m3"):
    dtype, down = {"e4m3": (ml_dtypes.float8_e4m3fn, 7), "e5m2": (ml_dtypes.float8_e5m2, 14)}[fmt]
    v = np.moveaxis(np.asarray(x, np.float32).astype(ml_dtypes.bfloat16).astype(np.float64), axis, -1)
    blocks = v.reshape(v.shape[:-1] + (-1, 32))
    amax = np.abs(blocks).max(-1, keepdims=True)
    byte = np.maximum(np.where(amax > 0, np.frexp(amax)[1] - 1 + 127, 0) - down, 1)
    scale = np.exp2(byte - 127.0)
    codes = (blocks / scale).astype(np.float32).astype(dtype).astype(np.float64)
    return np.moveaxis((codes * scale).reshape(v.shape), -1, axis)


WIDE = False


def mx_kscale(k):
    if not WIDE:
        return np.ones(k)
    levels = np.array([24, -24, 12, -12, 0])
    if k % 512:
        return np.exp2(np.random.permutation(np.resize(levels, k // 32))).repeat(32)
    a = np.empty((k // 512, 16))
    for p in range(k // 512):
        a[p, :8] = np.random.permutation(np.resize(levels, 8))
        for g in range(8):
            far = levels[np.abs(levels - a[p, g]) >= 10]
            a[p, g + 8] = far[np.random.randint(len(far))]
    return np.exp2(a.ravel()).repeat(32)


def f64(x):
    return np.asarray(x).astype(np.float64)


def striped8(idx):
    return np.concatenate([v.reshape(-1, 16).T for v in idx]).astype(np.uint16)


def unstriped8(offs):
    return np.stack([offs[16 * g:16 * g + 16].T.reshape(-1) for g in range(8)]).astype(np.int64)


E2M1 = np.array([0.0, 0.5, 1.0, 1.5, 2.0, 3.0, 4.0, 6.0, -0.0, -0.5, -1.0, -1.5, -2.0, -3.0, -4.0, -6.0])


def pack_weight(w, fmt):
    k, n = w.shape
    w = f64(np.asarray(w, np.float32).astype(ml_dtypes.bfloat16)).reshape(k // 32, 32, n)
    amax = np.abs(w).max(1)
    if fmt == "e4m3":
        byte = np.frexp(amax)[1] - 1 + 127 - 7
    else:
        mant, ex = np.frexp(amax / 6.0)
        byte = np.where(mant > 0.5, ex, ex - 1) + 127
    byte = np.clip(np.where(amax > 0, byte, 1), 1, 254)
    scaled = (w * np.exp2(127.0 - byte)[:, None, :]).reshape(k, n).astype(np.float32)
    by_word = np.ascontiguousarray(scaled.reshape(k // 512, 128, 4, n).transpose(0, 1, 3, 2))
    if fmt == "e4m3":
        words = by_word.astype(ml_dtypes.float8_e4m3fn).view(np.uint8)
    else:
        c = by_word.astype(ml_dtypes.float4_e2m1fn).view(np.uint8) & 0xF
        words = (c[..., 0::2] | (c[..., 1::2] << 4)).reshape(k // 512, 128, 2 * n)
    return np.ascontiguousarray(words), np.ascontiguousarray(byte.astype(np.uint8).reshape(k // 512, 16, n))


def unpack_weight(words, scales, fmt):
    g, _, n = scales.shape
    words = np.ascontiguousarray(words).reshape(g, 128, n, -1)
    if fmt == "e4m3":
        vals = words.view(ml_dtypes.float8_e4m3fn).astype(np.float64)
    else:
        nib = np.empty((g, 128, n, 4), np.uint8)
        nib[..., 0::2] = words & 0xF
        nib[..., 1::2] = words >> 4
        vals = E2M1[nib]
    vals = vals * np.repeat(np.exp2(scales.astype(np.float64) - 127.0), 8, axis=1)[..., None]
    return vals.transpose(0, 1, 3, 2).reshape(g * 512, n)


def planes(y):
    n, m = y.shape
    v = y.astype(np.float32).astype(ml_dtypes.bfloat16).astype(np.float64).reshape(n // 32, 32, m)
    top = np.abs(v).max(1)
    byte = np.clip(np.where(top > 0, np.frexp(top)[1] - 1 + 127 - 7, 1), 1, 254)
    codes = (v * np.exp2(127.0 - byte)[:, None, :]).reshape(n, m).astype(np.float32).astype(ml_dtypes.float8_e4m3fn).view(np.uint8)
    words = codes.reshape(n // 512, 128, 4, m).transpose(0, 1, 3, 2)
    return np.ascontiguousarray(words), np.ascontiguousarray(byte.astype(np.uint8).reshape(n // 512, 16, m))


def sigm(f):
    return 1.0 / (1.0 + np.exp(-np.maximum(f, -700.0)))


K, N, T, J = 1024, 512, 2048, 1024


def setup_inputs():
    n = np.random.standard_normal
    s = mx_kscale(K)[:, None]
    p_wk = pack_weight(n((K, N)) / np.sqrt(K) / s, "e2m1")
    p_wv = pack_weight(n((K, N)) / np.sqrt(K) / s, "e4m3")
    return {
        "xT": (n((K, T)) * s).astype(np.float32),
        "wgt": np.repeat(np.random.uniform(0.5, 2.0, (8, J)), 16, axis=0).astype(np.float32),
        "wk_words": p_wk[0],
        "wk_scales": p_wk[1],
        "wv_words": p_wv[0],
        "wv_scales": p_wv[1],
        "bg": (0.3 * n(N) - 1.0).astype(np.float32),
        "res": (n((N, J))).astype(np.float32),
        "offs": striped8(np.stack([np.random.permutation(T)[:J] for _ in range(8)])),
    }


def reference(xT, wgt, wk_words, wk_scales, wv_words, wv_scales, bg, res, offs):
    idx = unstriped8(offs)
    rows = np.arange(K)
    xg = f64(wgt)[rows // 4 % 128] * f64(xT)[rows[:, None], idx[rows % 512 // 64]]
    xT_ = mxq(xg, 0, "e4m3")
    wk_ = unpack_weight(wk_words, wk_scales, "e2m1")
    wv_ = unpack_weight(wv_words, wv_scales, "e4m3")
    ke = wk_.T @ xT_
    ve = wv_.T @ xT_
    gate = sigm(ke + f64(bg)[:, None])
    out_0 = f64(res) + gate * (np.maximum(ve, 0.0) - f64(res))
    return (out_0,) + planes(out_0)

@@ -1,0 +1,179 @@
+from contextlib import ExitStack
+
+import concourse.mybir as mybir
+
+K, N, T, J = 1024, 512, 2048, 1024
+FLOPS = 2 * 2 * K * N * J
+
+F32 = mybir.dt.float32
+BF16 = mybir.dt.bfloat16
+I32 = mybir.dt.int32
+U32 = mybir.dt.uint32
+U16 = mybir.dt.uint16
+U8 = mybir.dt.uint8
+FP8X4 = mybir.dt.float8_e4m3fn_x4
+FP4X4 = mybir.dt.float4_e2m1fn_x4
+ALU = mybir.AluOpType
+ACT = mybir.ActivationFunctionType
+
+P = 128
+PACK = 4
+PASSES = K // (P * PACK)
+HALF = 512
+CH = 256
+NCH = J // CH
+
+
+def tile_list_hwayreluP_kernel(
+    tc, xT, wgt, wk_words, wk_scales, wv_words, wv_scales, bg, res, offs, out_0, out_1, out_2
+):
+    nc = tc.nc
+    with ExitStack() as ctx:
+        keep = ctx.enter_context(tc.tile_pool(name="keep", bufs=1))
+        psum = ctx.enter_context(tc.psum_pool(name="psum", bufs=1))
+
+        offsets = keep.tile([P, J // 16], U16, name="offsets")
+        nc.sync.dma_start(offsets[:], offs)
+
+        wk_raw = keep.tile([P, PASSES, 2 * N], U8, name="wk_raw")
+        nc.sync.dma_start(wk_raw[:].bitcast(I32), wk_words.rearrange("a p b -> p a b").bitcast(I32))
+
+        x_rows = xT.rearrange("(a p i) t -> a i p t", a=PASSES, i=PACK)
+        planes = [[keep.tile([P, T], F32, name=f"x{a}{i}") for i in range(PACK)] for a in range(PASSES)]
+        wgt_sb = keep.tile([P, J], F32, name="wgt_sb")
+        wv_raw = keep.tile([P, PASSES, N], I32, name="wv_raw")
+        sc_raw = keep.tile([P, PASSES, N], U8, name="sc_raw")
+        nc.vector.memset(sc_raw[:].bitcast(I32), 0)
+        bias = keep.tile([P, PACK], F32, name="bias")
+
+        def load_scales(q):
+            for row0, scales in ((0, wk_scales), (4, wv_scales)):
+                nc.sync.dma_start(
+                    sc_raw[32 * q + row0 : 32 * q + row0 + 4].bitcast(I32),
+                    scales[:, 4 * q : 4 * q + 4, :].rearrange("a r n -> r a n").bitcast(I32),
+                )
+
+        nc.sync.dma_start(wgt_sb[:, 0:HALF], wgt[:, 0:HALF])
+        nc.sync.dma_start(planes[0][0][:], x_rows[0, 0])
+        nc.sync.dma_start(wgt_sb[:, HALF:J], wgt[:, HALF:J])
+        for i in range(1, PACK):
+            nc.sync.dma_start(planes[0][i][:], x_rows[0, i])
+            load_scales(i - 1)
+        nc.sync.dma_start(planes[1][0][:], x_rows[1, 0])
+        load_scales(PACK - 1)
+        nc.sync.dma_start(wv_raw[:], wv_words.rearrange("a p n i -> p a (n i)").bitcast(I32))
+        nc.sync.dma_start(bias[:], bg.rearrange("(p t) -> p t", t=PACK))
+        for i in range(1, PACK):
+            nc.sync.dma_start(planes[1][i][:], x_rows[1, i])
+        res_rows = res.rearrange("(p t) j -> p t j", t=PACK)
+        res_sb = [keep.tile([P, PACK, CH], F32, name=f"res{c}") for c in range(NCH)]
+        for c in range(NCH):
+            nc.sync.dma_start(res_sb[c][:], res_rows[:, :, c * CH : (c + 1) * CH])
+
+        wk_d = keep.tile([P, PASSES, 2 * N], U8, name="wk_d", align_bytes=64)
+        for a in range(PASSES):
+            nc.vector.tensor_copy(
+                wk_d[:, a, :].rearrange("p (t mb mi b) -> p mb t mi b", t=PACK, mi=8, b=2),
+                wk_raw[:, a, :].rearrange("p (mb mi t b) -> p mb t mi b", t=PACK, mi=8, b=2),
+            )
+        wv_d = keep.tile([P, PASSES, N], I32, name="wv_d", align_bytes=64)
+        nc.vector.tensor_copy(
+            wv_d[:].rearrange("p a (t mb mi) -> p a mb t mi", t=PACK, mi=4),
+            wv_raw[:].rearrange("p a (mb mi t) -> p a mb t mi", t=PACK, mi=4),
+        )
+        sc_d = keep.tile([P, PASSES, N], U8, name="sc_d", align_bytes=64)
+        nc.vector.tensor_copy(
+            sc_d[:].rearrange("p a (t mb mi) -> p a mb t mi", t=PACK, mi=16),
+            sc_raw[:].rearrange("p a (mb mi t) -> p a mb t mi", t=PACK, mi=16),
+        )
+
+        xg_codes = [[keep.tile([P, HALF], U32, name=f"xc{a}{h}", align_bytes=64) for h in range(2)] for a in range(PASSES)]
+        xg_scales = [[keep.tile([P, HALF], U8, name=f"xs{a}{h}", align_bytes=64) for h in range(2)] for a in range(PASSES)]
+
+        def gather(dst, a, i, j0, j1):
+            nc.vector.tensor_tensor(
+                dst, planes[a][i][:].indirect(offsets[:, j0 // 16 : j1 // 16]), wgt_sb[:, j0:j1], ALU.mult
+            )
+
+        def weave(dst, src):
+            nc.scalar.copy(
+                dst.rearrange("p (c i t) -> p c t i", i=4, t=PACK),
+                src.rearrange("p t (c i) -> p c t i", i=4),
+            )
+
+        def quant_x(a, src, j0, j1):
+            h, s0 = divmod(j0, HALF)
+            woven = keep.tile([P, PACK * (j1 - j0)], BF16, name=f"xw{a}_{j0}", align_bytes=64)
+            weave(woven[:], src)
+            nc.vector.quantize_mx(
+                xg_codes[a][h][:, s0 : s0 + j1 - j0].bitcast(FP8X4),
+                xg_scales[a][h][:, s0 : s0 + j1 - j0],
+                woven[:],
+            )
+
+        first = keep.tile([P, PACK, J], F32, name="first")
+        for h in range(2):
+            gather(first[:, 0, h * HALF : (h + 1) * HALF], 0, 0, h * HALF, (h + 1) * HALF)
+        for i in range(1, PACK):
+            gather(first[:, i, :], 0, i, 0, J)
+        for h in range(2):
+            quant_x(0, first[:, :, h * HALF : (h + 1) * HALF], h * HALF, (h + 1) * HALF)
+        second = keep.tile([P, PACK, J], F32, name="second")
+        for i in range(PACK - 1):
+            gather(second[:, i, :], 1, i, 0, J)
+        for c in range(NCH):
+            gather(second[:, PACK - 1, c * CH : (c + 1) * CH], 1, PACK - 1, c * CH, (c + 1) * CH)
+            quant_x(1, second[:, :, c * CH : (c + 1) * CH], c * CH, (c + 1) * CH)
+
+        out_rows = out_0.rearrange("(p t) j -> p t j", t=PACK)
+        out_words = out_1[0].rearrange("p j i -> p (j i)").bitcast(I32)
+        y_scales = keep.tile([P, J], U8, name="y_scales", align_bytes=64)
+        for h in range(2):
+            ke = [psum.tile([P, HALF], F32, name=f"ke{t}") for t in range(PACK)]
+            ve = [psum.tile([P, HALF], F32, name=f"ve{t}") for t in range(PACK)]
+            for a in range(PASSES):
+                for t in range(PACK):
+                    cols = slice(t * P, (t + 1) * P)
+                    nc.tensor.matmul_mx(
+                        ke[t][:],
+                        lhsT=wk_d[:, a, 2 * t * P : 2 * (t + 1) * P].bitcast(FP4X4),
+                        lhsT_scale=sc_d[:, a, cols],
+                        rhs=xg_codes[a][h][:].bitcast(FP8X4),
+                        rhs_scale=xg_scales[a][h][:],
+                        start=(a == 0),
+                        stop=(a == PASSES - 1),
+                    )
+                    nc.tensor.matmul_mx(
+                        ve[t][:],
+                        lhsT=wv_d[:, a, cols].bitcast(FP8X4),
+                        lhsT_scale=sc_d[4:P, a, cols],
+                        rhs=xg_codes[a][h][:].bitcast(FP8X4),
+                        rhs_scale=xg_scales[a][h][:],
+                        start=(a == 0),
+                        stop=(a == PASSES - 1),
+                    )
+            gate = [keep.tile([P, PACK, CH], F32, name=f"gate{h}{s}") for s in range(2)]
+            diff = [keep.tile([P, PACK, CH], F32, name=f"diff{h}{s}") for s in range(2)]
+            for s in range(2):
+                cs = slice(s * CH, (s + 1) * CH)
+                for t in range(PACK):
+                    nc.scalar.activation(gate[s][:, t, :], ke[t][:, cs], ACT.Sigmoid, bias=bias[:, t : t + 1])
+                    nc.vector.scalar_tensor_tensor(
+                        diff[s][:, t, :], ve[t][:, cs], 0.0, res_sb[2 * h + s][:, t, :], ALU.max, ALU.subtract
+                    )
+            for s in range(2):
+                c = 2 * h + s
+                js = slice(c * CH, (c + 1) * CH)
+                step = keep.tile([P, PACK, CH], F32, name=f"step{c}")
+                nc.vector.tensor_tensor(step[:], diff[s][:], gate[s][:], ALU.mult)
+                y = keep.tile([P, PACK, CH], F32, name=f"y{c}")
+                nc.vector.tensor_tensor(y[:], step[:], res_sb[c][:], ALU.add)
+                nc.sync.dma_start(out_rows[:, :, js], y[:])
+                y_woven = keep.tile([P, PACK * CH], BF16, name=f"yw{c}", align_bytes=64)
+                weave(y_woven[:], y[:])
+                y_codes = keep.tile([P, CH], U32, name=f"yc{c}", align_bytes=64)
+                nc.vector.quantize_mx(y_codes[:].bitcast(FP8X4), y_scales[:, js], y_woven[:])
+                nc.sync.dma_start(out_words[:, js], y_codes[:].bitcast(I32))
+        for q in range(4):
+            eng = nc.scalar if q % 2 else nc.sync
+            eng.dma_start(out_2[0, 4 * q : 4 * q + 4, :].bitcast(I32), y_scales[32 * q : 32 * q + 4, :].bitcast(I32))

@@ -19,9 +19,18 @@ ACT = mybir.ActivationFunctionType
 P = 128
 PACK = 4
 PASSES = K // (P * PACK)
-HALF = 512
-CH = 256
-NCH = J // CH
+GROUP = 16
+QUADS = 4
+WV_ROW = 4
+HALF = J // 2
+BANK = 512
+BANKS = 8
+WIDTHS = [128, 128, 256, 256, 128, 128]
+STARTS = [sum(WIDTHS[:c]) for c in range(len(WIDTHS))]
+CHUNKS = len(WIDTHS)
+LAST = CHUNKS - 1
+EARLY = 3
+AHEAD = 2
 
 
 def tile_list_hwayreluP_kernel(
@@ -30,26 +39,32 @@ def tile_list_hwayreluP_kernel(
     nc = tc.nc
     with ExitStack() as ctx:
         keep = ctx.enter_context(tc.tile_pool(name="keep", bufs=1))
-        psum = ctx.enter_context(tc.psum_pool(name="psum", bufs=1))
+        psum = ctx.enter_context(tc.psum_pool(name="psum", bufs=BANKS))
 
-        offsets = keep.tile([P, J // 16], U16, name="offsets")
+        def chunk(c):
+            return slice(STARTS[c], STARTS[c] + WIDTHS[c])
+
+        offsets = keep.tile([P, J // GROUP], U16, name="offsets")
         nc.sync.dma_start(offsets[:], offs)
-
         wk_raw = keep.tile([P, PASSES, 2 * N], U8, name="wk_raw")
         nc.sync.dma_start(wk_raw[:].bitcast(I32), wk_words.rearrange("a p b -> p a b").bitcast(I32))
 
         x_rows = xT.rearrange("(a p i) t -> a i p t", a=PASSES, i=PACK)
         planes = [[keep.tile([P, T], F32, name=f"x{a}{i}") for i in range(PACK)] for a in range(PASSES)]
         wgt_sb = keep.tile([P, J], F32, name="wgt_sb")
-        wv_raw = keep.tile([P, PASSES, N], I32, name="wv_raw")
-        sc_raw = keep.tile([P, PASSES, N], U8, name="sc_raw")
-        nc.vector.memset(sc_raw[:].bitcast(I32), 0)
+        wv_raw = keep.tile([P, PASSES, N], I32, name="wv_raw", tag="wv_then_codes", align_bytes=64)
+        scale_raw = keep.tile([P, PASSES, N], U8, name="scale_raw")
+        nc.gpsimd.memset(scale_raw[:].bitcast(I32), 0)
         bias = keep.tile([P, PACK], F32, name="bias")
+        warm_in = keep.tile([P, 8], F32, name="warm_in")
+        nc.gpsimd.memset(warm_in[:], 0.0)
+        warm_out = keep.tile([P, 8], F32, name="warm_out")
+        nc.scalar.activation(warm_out[:], warm_in[:], ACT.Sigmoid)
 
         def load_scales(q):
-            for row0, scales in ((0, wk_scales), (4, wv_scales)):
+            for row0, scales in ((0, wk_scales), (WV_ROW, wv_scales)):
                 nc.sync.dma_start(
-                    sc_raw[32 * q + row0 : 32 * q + row0 + 4].bitcast(I32),
+                    scale_raw[32 * q + row0 : 32 * q + row0 + 4].bitcast(I32),
                     scales[:, 4 * q : 4 * q + 4, :].rearrange("a r n -> r a n").bitcast(I32),
                 )
 
@@ -58,122 +73,178 @@ def tile_list_hwayreluP_kernel(
         nc.sync.dma_start(wgt_sb[:, HALF:J], wgt[:, HALF:J])
         for i in range(1, PACK):
             nc.sync.dma_start(planes[0][i][:], x_rows[0, i])
-            load_scales(i - 1)
-        nc.sync.dma_start(planes[1][0][:], x_rows[1, 0])
-        load_scales(PACK - 1)
+        for i in range(QUADS // 2):
+            load_scales(2 * i)
+            load_scales(2 * i + 1)
+            nc.sync.dma_start(planes[1][i][:], x_rows[1, i])
         nc.sync.dma_start(wv_raw[:], wv_words.rearrange("a p n i -> p a (n i)").bitcast(I32))
         nc.sync.dma_start(bias[:], bg.rearrange("(p t) -> p t", t=PACK))
-        for i in range(1, PACK):
+        for i in range(QUADS // 2, PACK):
             nc.sync.dma_start(planes[1][i][:], x_rows[1, i])
         res_rows = res.rearrange("(p t) j -> p t j", t=PACK)
-        res_sb = [keep.tile([P, PACK, CH], F32, name=f"res{c}") for c in range(NCH)]
-        for c in range(NCH):
-            nc.sync.dma_start(res_sb[c][:], res_rows[:, :, c * CH : (c + 1) * CH])
+        res_sb = [keep.tile([P, PACK, WIDTHS[c]], F32, name=f"res{c}") for c in range(CHUNKS)]
+        for c in range(CHUNKS):
+            nc.sync.dma_start(res_sb[c][:], res_rows[:, :, chunk(c)])
 
-        wk_d = keep.tile([P, PASSES, 2 * N], U8, name="wk_d", align_bytes=64)
+        wk_dealt = keep.tile([P, PASSES, 2 * N], U8, name="wk_dealt", align_bytes=64)
         for a in range(PASSES):
             nc.vector.tensor_copy(
-                wk_d[:, a, :].rearrange("p (t mb mi b) -> p mb t mi b", t=PACK, mi=8, b=2),
+                wk_dealt[:, a, :].rearrange("p (t mb mi b) -> p mb t mi b", t=PACK, mi=8, b=2),
                 wk_raw[:, a, :].rearrange("p (mb mi t b) -> p mb t mi b", t=PACK, mi=8, b=2),
             )
-        wv_d = keep.tile([P, PASSES, N], I32, name="wv_d", align_bytes=64)
+        wv_dealt = keep.tile([P, PASSES, N], I32, name="wv_dealt", align_bytes=64)
         nc.vector.tensor_copy(
-            wv_d[:].rearrange("p a (t mb mi) -> p a mb t mi", t=PACK, mi=4),
+            wv_dealt[:].rearrange("p a (t mb mi) -> p a mb t mi", t=PACK, mi=4),
             wv_raw[:].rearrange("p a (mb mi t) -> p a mb t mi", t=PACK, mi=4),
         )
-        sc_d = keep.tile([P, PASSES, N], U8, name="sc_d", align_bytes=64)
+        scale_dealt = keep.tile([P, PASSES, N], U8, name="scale_dealt", align_bytes=64)
         nc.vector.tensor_copy(
-            sc_d[:].rearrange("p a (t mb mi) -> p a mb t mi", t=PACK, mi=16),
-            sc_raw[:].rearrange("p a (mb mi t) -> p a mb t mi", t=PACK, mi=16),
+            scale_dealt[:].rearrange("p a (t mb mi) -> p a mb t mi", t=PACK, mi=16),
+            scale_raw[:].rearrange("p a (mb mi t) -> p a mb t mi", t=PACK, mi=16),
         )
 
-        xg_codes = [[keep.tile([P, HALF], U32, name=f"xc{a}{h}", align_bytes=64) for h in range(2)] for a in range(PASSES)]
-        xg_scales = [[keep.tile([P, HALF], U8, name=f"xs{a}{h}", align_bytes=64) for h in range(2)] for a in range(PASSES)]
+        def gather(dst, a, i, cols):
+            picks = offsets[:, cols.start // GROUP : cols.stop // GROUP]
+            nc.vector.tensor_tensor(dst, planes[a][i][:].indirect(picks), wgt_sb[:, cols], ALU.mult)
 
-        def gather(dst, a, i, j0, j1):
-            nc.vector.tensor_tensor(
-                dst, planes[a][i][:].indirect(offsets[:, j0 // 16 : j1 // 16]), wgt_sb[:, j0:j1], ALU.mult
-            )
-
-        def weave(dst, src):
-            nc.scalar.copy(
+        def weave(copy, dst, src):
+            copy(
                 dst.rearrange("p (c i t) -> p c t i", i=4, t=PACK),
                 src.rearrange("p t (c i) -> p c t i", i=4),
             )
 
-        def quant_x(a, src, j0, j1):
-            h, s0 = divmod(j0, HALF)
-            woven = keep.tile([P, PACK * (j1 - j0)], BF16, name=f"xw{a}_{j0}", align_bytes=64)
-            weave(woven[:], src)
-            nc.vector.quantize_mx(
-                xg_codes[a][h][:, s0 : s0 + j1 - j0].bitcast(FP8X4),
-                xg_scales[a][h][:, s0 : s0 + j1 - j0],
-                woven[:],
-            )
-
-        first = keep.tile([P, PACK, J], F32, name="first")
-        for h in range(2):
-            gather(first[:, 0, h * HALF : (h + 1) * HALF], 0, 0, h * HALF, (h + 1) * HALF)
+        halves = [slice(0, HALF), slice(HALF, J)]
+        picked0 = keep.tile([P, PACK, J], F32, name="picked0")
+        for cols in halves:
+            gather(picked0[:, 0, cols], 0, 0, cols)
         for i in range(1, PACK):
-            gather(first[:, i, :], 0, i, 0, J)
-        for h in range(2):
-            quant_x(0, first[:, :, h * HALF : (h + 1) * HALF], h * HALF, (h + 1) * HALF)
-        second = keep.tile([P, PACK, J], F32, name="second")
+            gather(picked0[:, i, :], 0, i, slice(0, J))
+        woven0 = keep.tile([P, PACK * J], BF16, name="woven0", align_bytes=64)
+        for cols in halves:
+            weave(nc.scalar.copy, woven0[:, PACK * cols.start : PACK * cols.stop], picked0[:, :, cols])
+        codes0 = keep.tile([P, J], U32, name="codes0", tag="wv_then_codes", align_bytes=64)
+        scales0 = keep.tile([P, J], U8, name="scales0", align_bytes=64)
+        nc.vector.quantize_mx(codes0[:].bitcast(FP8X4), scales0[:], woven0[:])
+
+        picked1 = keep.tile([P, PACK, STARTS[LAST]], F32, name="picked1")
         for i in range(PACK - 1):
-            gather(second[:, i, :], 1, i, 0, J)
-        for c in range(NCH):
-            gather(second[:, PACK - 1, c * CH : (c + 1) * CH], 1, PACK - 1, c * CH, (c + 1) * CH)
-            quant_x(1, second[:, :, c * CH : (c + 1) * CH], c * CH, (c + 1) * CH)
+            gather(picked1[:, i, :], 1, i, slice(0, STARTS[LAST]))
+        for c in range(LAST):
+            gather(picked1[:, PACK - 1, chunk(c)], 1, PACK - 1, chunk(c))
 
         out_rows = out_0.rearrange("(p t) j -> p t j", t=PACK)
         out_words = out_1[0].rearrange("p j i -> p (j i)").bitcast(I32)
         y_scales = keep.tile([P, J], U8, name="y_scales", align_bytes=64)
-        for h in range(2):
-            ke = [psum.tile([P, HALF], F32, name=f"ke{t}") for t in range(PACK)]
-            ve = [psum.tile([P, HALF], F32, name=f"ve{t}") for t in range(PACK)]
-            for a in range(PASSES):
-                for t in range(PACK):
-                    cols = slice(t * P, (t + 1) * P)
+        picked_of = {c: picked1[:, :, chunk(c)] for c in range(LAST)}
+        operand1, banks, gate, diff, step, y = {}, {}, {}, {}, {}, {}
+
+        def quantise_pass1(c):
+            woven = keep.tile([P, PACK * WIDTHS[c]], BF16, name=f"woven1_{c}", tag=f"woven1_{c}", align_bytes=64)
+            weave(nc.scalar.copy, woven[:], picked_of[c])
+            codes = keep.tile([P, WIDTHS[c]], U32, name=f"codes1_{c}", align_bytes=64)
+            scales = keep.tile([P, WIDTHS[c]], U8, name=f"scales1_{c}", align_bytes=64)
+            nc.vector.quantize_mx(codes[:].bitcast(FP8X4), scales[:], woven[:])
+            operand1[c] = (codes, scales)
+
+        def gather_last_chunk():
+            picked = keep.tile([P, PACK, WIDTHS[LAST]], F32, name="picked_last", tag="woven1_0", align_bytes=64)
+            for i in range(PACK):
+                gather(picked[:, i, :], 1, i, chunk(LAST))
+            picked_of[LAST] = picked[:]
+
+        def multiply(c, a):
+            width = WIDTHS[c]
+            per_bank = BANK // width
+            if a == 0:
+                banks[c] = [
+                    (psum.tile([P, BANK], F32, name="ke", tag="sum"), psum.tile([P, BANK], F32, name="ve", tag="sum"))
+                    for b in range(PACK // per_bank)
+                ]
+                codes, scales, j0 = codes0, scales0, STARTS[c]
+            else:
+                codes, scales, j0 = operand1[c][0], operand1[c][1], 0
+            for b, (ke, ve) in enumerate(banks[c]):
+                for u in range(per_bank):
+                    t = b * per_bank + u
+                    for s in range(0, width, P):
+                        nc.tensor.matmul_mx(
+                            ke[:, u * width + s : u * width + s + P],
+                            lhsT=wk_dealt[:, a, 2 * t * P : 2 * (t + 1) * P].bitcast(FP4X4),
+                            lhsT_scale=scale_dealt[:, a, t * P : (t + 1) * P],
+                            rhs=codes[:, j0 + s : j0 + s + P].bitcast(FP8X4),
+                            rhs_scale=scales[:, j0 + s : j0 + s + P],
+                            start=(a == 0 and u == 0 and s == 0),
+                            stop=(a == PASSES - 1 and u == per_bank - 1 and s == width - P),
+                        )
+                for u in range(per_bank):
+                    t = b * per_bank + u
                     nc.tensor.matmul_mx(
-                        ke[t][:],
-                        lhsT=wk_d[:, a, 2 * t * P : 2 * (t + 1) * P].bitcast(FP4X4),
-                        lhsT_scale=sc_d[:, a, cols],
-                        rhs=xg_codes[a][h][:].bitcast(FP8X4),
-                        rhs_scale=xg_scales[a][h][:],
-                        start=(a == 0),
-                        stop=(a == PASSES - 1),
+                        ve[:, u * width : (u + 1) * width],
+                        lhsT=wv_dealt[:, a, t * P : (t + 1) * P].bitcast(FP8X4),
+                        lhsT_scale=scale_dealt[WV_ROW:P, a, t * P : (t + 1) * P],
+                        rhs=codes[:, j0 : j0 + width].bitcast(FP8X4),
+                        rhs_scale=scales[:, j0 : j0 + width],
+                        start=(a == 0 and u == 0),
+                        stop=(a == PASSES - 1 and u == per_bank - 1),
                     )
-                    nc.tensor.matmul_mx(
-                        ve[t][:],
-                        lhsT=wv_d[:, a, cols].bitcast(FP8X4),
-                        lhsT_scale=sc_d[4:P, a, cols],
-                        rhs=xg_codes[a][h][:].bitcast(FP8X4),
-                        rhs_scale=xg_scales[a][h][:],
-                        start=(a == 0),
-                        stop=(a == PASSES - 1),
+
+        def read_banks(c):
+            width = WIDTHS[c]
+            per_bank = BANK // width
+            gate[c] = keep.tile([P, PACK, width], F32, name=f"gate{c}")
+            diff[c] = keep.tile([P, PACK, width], F32, name=f"diff{c}")
+            for b, (ke, ve) in enumerate(banks[c]):
+                for u in range(per_bank):
+                    t = b * per_bank + u
+                    nc.scalar.activation(
+                        gate[c][:, t, :], ke[:, u * width : (u + 1) * width], ACT.Sigmoid, bias=bias[:, t : t + 1]
                     )
-            gate = [keep.tile([P, PACK, CH], F32, name=f"gate{h}{s}") for s in range(2)]
-            diff = [keep.tile([P, PACK, CH], F32, name=f"diff{h}{s}") for s in range(2)]
-            for s in range(2):
-                cs = slice(s * CH, (s + 1) * CH)
-                for t in range(PACK):
-                    nc.scalar.activation(gate[s][:, t, :], ke[t][:, cs], ACT.Sigmoid, bias=bias[:, t : t + 1])
-                    nc.vector.scalar_tensor_tensor(
-                        diff[s][:, t, :], ve[t][:, cs], 0.0, res_sb[2 * h + s][:, t, :], ALU.max, ALU.subtract
-                    )
-            for s in range(2):
-                c = 2 * h + s
-                js = slice(c * CH, (c + 1) * CH)
-                step = keep.tile([P, PACK, CH], F32, name=f"step{c}")
-                nc.vector.tensor_tensor(step[:], diff[s][:], gate[s][:], ALU.mult)
-                y = keep.tile([P, PACK, CH], F32, name=f"y{c}")
-                nc.vector.tensor_tensor(y[:], step[:], res_sb[c][:], ALU.add)
-                nc.sync.dma_start(out_rows[:, :, js], y[:])
-                y_woven = keep.tile([P, PACK * CH], BF16, name=f"yw{c}", align_bytes=64)
-                weave(y_woven[:], y[:])
-                y_codes = keep.tile([P, CH], U32, name=f"yc{c}", align_bytes=64)
-                nc.vector.quantize_mx(y_codes[:].bitcast(FP8X4), y_scales[:, js], y_woven[:])
-                nc.sync.dma_start(out_words[:, js], y_codes[:].bitcast(I32))
-        for q in range(4):
-            eng = nc.scalar if q % 2 else nc.sync
-            eng.dma_start(out_2[0, 4 * q : 4 * q + 4, :].bitcast(I32), y_scales[32 * q : 32 * q + 4, :].bitcast(I32))
+                rows = slice(b * per_bank, (b + 1) * per_bank)
+                nc.vector.scalar_tensor_tensor(
+                    diff[c][:, rows, :].rearrange("p t j -> p (t j)"),
+                    ve[:],
+                    0.0,
+                    res_sb[c][:, rows, :].rearrange("p t j -> p (t j)"),
+                    ALU.max,
+                    ALU.subtract,
+                )
+
+        def apply_gate(c):
+            step[c] = keep.tile([P, PACK, WIDTHS[c]], F32, name=f"step{c}")
+            nc.vector.tensor_tensor(step[c][:], diff[c][:], gate[c][:], ALU.mult)
+
+        def add_res(c):
+            y[c] = keep.tile([P, PACK, WIDTHS[c]], F32, name=f"y{c}")
+            nc.vector.tensor_tensor(y[c][:], step[c][:], res_sb[c][:], ALU.add)
+            nc.sync.dma_start(out_rows[:, :, chunk(c)], y[c][:])
+
+        def hand_on(c):
+            y_woven = keep.tile([P, PACK * WIDTHS[c]], BF16, name=f"y_woven{c}", align_bytes=64)
+            weave(nc.vector.tensor_copy if c == LAST else nc.scalar.copy, y_woven[:], y[c][:])
+            y_codes = keep.tile([P, WIDTHS[c]], U32, name=f"y_codes{c}", align_bytes=64)
+            nc.vector.quantize_mx(y_codes[:].bitcast(FP8X4), y_scales[:, chunk(c)], y_woven[:])
+            nc.sync.dma_start(out_words[:, chunk(c)], y_codes[:].bitcast(I32))
+
+        for c in range(EARLY):
+            multiply(c, 0)
+        quantise_pass1(0)
+        gather_last_chunk()
+        for c in range(1, AHEAD):
+            quantise_pass1(c)
+        for c in range(CHUNKS + 1):
+            if c < CHUNKS:
+                if c >= EARLY:
+                    multiply(c, 0)
+                multiply(c, 1)
+                read_banks(c)
+            if c + AHEAD < CHUNKS:
+                quantise_pass1(c + AHEAD)
+            if c >= 1:
+                add_res(c - 1)
+            if c < CHUNKS:
+                apply_gate(c)
+            if c >= 1:
+                hand_on(c - 1)
+        for q in range(QUADS):
+            queue = nc.scalar if q % 2 else nc.sync
+            queue.dma_start(out_2[0, 4 * q : 4 * q + 4, :].bitcast(I32), y_scales[32 * q : 32 * q + 4, :].bitcast(I32))

@@ -25,12 +25,13 @@ WV_ROW = 4
 HALF = J // 2
 BANK = 512
 BANKS = 8
-WIDTHS = [128, 128, 256, 256, 128, 128]
+WIDTHS = [128, 256, 256, 256, 128]
 STARTS = [sum(WIDTHS[:c]) for c in range(len(WIDTHS))]
 CHUNKS = len(WIDTHS)
 LAST = CHUNKS - 1
-EARLY = 3
+EARLY = 2
 AHEAD = 2
+GPSIMD_SHARE = 320
 
 
 def tile_list_hwayreluP_kernel(
@@ -215,7 +216,11 @@ def tile_list_hwayreluP_kernel(
 
         def add_res(c):
             y[c] = keep.tile([P, PACK, WIDTHS[c]], F32, name=f"y{c}")
-            nc.vector.tensor_tensor(y[c][:], step[c][:], res_sb[c][:], ALU.add)
+            flat = [tile[:].rearrange("p t j -> p (t j)") for tile in (y[c], step[c], res_sb[c])]
+            share = GPSIMD_SHARE if c < LAST and WIDTHS[c + 1] == max(WIDTHS) else 0
+            if share:
+                nc.gpsimd.tensor_tensor(*[ap[:, :share] for ap in flat], ALU.add)
+            nc.vector.tensor_tensor(*[ap[:, share:] for ap in flat], ALU.add)
             nc.sync.dma_start(out_rows[:, :, chunk(c)], y[c][:])
 
         def hand_on(c):
@@ -231,7 +236,7 @@ def tile_list_hwayreluP_kernel(
         gather_last_chunk()
         for c in range(1, AHEAD):
             quantise_pass1(c)
-        for c in range(CHUNKS + 1):
+        for c in range(CHUNKS + 2):
             if c < CHUNKS:
                 if c >= EARLY:
                     multiply(c, 0)
@@ -239,12 +244,12 @@ def tile_list_hwayreluP_kernel(
                 read_banks(c)
             if c + AHEAD < CHUNKS:
                 quantise_pass1(c + AHEAD)
-            if c >= 1:
+            if c >= 2:
+                hand_on(c - 2)
+            if 1 <= c <= CHUNKS:
                 add_res(c - 1)
             if c < CHUNKS:
                 apply_gate(c)
-            if c >= 1:
-                hand_on(c - 1)
         for q in range(QUADS):
             queue = nc.scalar if q % 2 else nc.sync
             queue.dma_start(out_2[0, 4 * q : 4 * q + 4, :].bitcast(I32), y_scales[32 * q : 32 * q + 4, :].bitcast(I32))

@@ -31,7 +31,7 @@ CHUNKS = len(WIDTHS)
 LAST = CHUNKS - 1
 EARLY = 2
 AHEAD = 2
-GPSIMD_SHARE = 320
+GPSIMD_SHARE = 352
 
 
 def tile_list_hwayreluP_kernel(
@@ -210,17 +210,27 @@ def tile_list_hwayreluP_kernel(
                     ALU.subtract,
                 )
 
+        def flat(tile):
+            return tile[:].rearrange("p t j -> p (t j)")
+
+        def gpsimd_share(c):
+            return GPSIMD_SHARE if c < LAST and WIDTHS[c + 1] == max(WIDTHS) else 0
+
         def apply_gate(c):
             step[c] = keep.tile([P, PACK, WIDTHS[c]], F32, name=f"step{c}")
-            nc.vector.tensor_tensor(step[c][:], diff[c][:], gate[c][:], ALU.mult)
+            operands = [flat(step[c]), flat(diff[c]), flat(gate[c])]
+            share = gpsimd_share(c)
+            if share:
+                nc.vector.tensor_tensor(*[ap[:, :share] for ap in operands], ALU.mult)
+            nc.vector.tensor_tensor(*[ap[:, share:] for ap in operands], ALU.mult)
 
         def add_res(c):
             y[c] = keep.tile([P, PACK, WIDTHS[c]], F32, name=f"y{c}")
-            flat = [tile[:].rearrange("p t j -> p (t j)") for tile in (y[c], step[c], res_sb[c])]
-            share = GPSIMD_SHARE if c < LAST and WIDTHS[c + 1] == max(WIDTHS) else 0
+            operands = [flat(y[c]), flat(step[c]), flat(res_sb[c])]
+            share = gpsimd_share(c)
             if share:
-                nc.gpsimd.tensor_tensor(*[ap[:, :share] for ap in flat], ALU.add)
-            nc.vector.tensor_tensor(*[ap[:, share:] for ap in flat], ALU.add)
+                nc.gpsimd.tensor_tensor(*[ap[:, :share] for ap in operands], ALU.add)
+            nc.vector.tensor_tensor(*[ap[:, share:] for ap in operands], ALU.add)
             nc.sync.dma_start(out_rows[:, :, chunk(c)], y[c][:])
 
         def hand_on(c):

@@ -1,6 +1,7 @@
 from contextlib import ExitStack
 
 import concourse.mybir as mybir
+from concourse.masks import make_identity
 
 K, N, T, J = 1024, 512, 2048, 1024
 FLOPS = 2 * 2 * K * N * J
@@ -23,6 +24,8 @@ GROUP = 16
 QUADS = 4
 WV_ROW = 4
 HALF = J // 2
+HEADS = P // GROUP
+PIECES = J // P
 BANK = 512
 BANKS = 8
 WIDTHS = [128, 256, 256, 256, 128]
@@ -31,7 +34,7 @@ CHUNKS = len(WIDTHS)
 LAST = CHUNKS - 1
 EARLY = 2
 AHEAD = 2
-GPSIMD_SHARE = 352
+GPSIMD_SHARE = {256: 384, 128: 128}
 
 
 def tile_list_hwayreluP_kernel(
@@ -45,15 +48,25 @@ def tile_list_hwayreluP_kernel(
         def chunk(c):
             return slice(STARTS[c], STARTS[c] + WIDTHS[c])
 
+        wgt_rows = keep.tile([P, P], F32, name="wgt_rows")
+        nc.gpsimd.memset(wgt_rows[HEADS * PIECES : P, :], 0.0)
+        nc.sync.dma_start(
+            wgt_rows[0 : HEADS * PIECES, :], wgt.rearrange("(g s) (r c) -> s g r c", s=GROUP, r=PIECES)[0]
+        )
+        identity = keep.tile([P, P], F32, name="identity")
+        make_identity(nc, identity[:])
         offsets = keep.tile([P, J // GROUP], U16, name="offsets")
         nc.sync.dma_start(offsets[:], offs)
         wk_raw = keep.tile([P, PASSES, 2 * N], U8, name="wk_raw")
         nc.sync.dma_start(wk_raw[:].bitcast(I32), wk_words.rearrange("a p b -> p a b").bitcast(I32))
 
         x_rows = xT.rearrange("(a p i) t -> a i p t", a=PASSES, i=PACK)
-        planes = [[keep.tile([P, T], F32, name=f"x{a}{i}") for i in range(PACK)] for a in range(PASSES)]
+        planes = [
+            [keep.tile([P, T], F32, name=f"x{a}{i}", tag=f"x{a}{i}", align_bytes=64) for i in range(PACK)]
+            for a in range(PASSES)
+        ]
         wgt_sb = keep.tile([P, J], F32, name="wgt_sb")
-        wv_raw = keep.tile([P, PASSES, N], I32, name="wv_raw", tag="wv_then_codes", align_bytes=64)
+        wv_raw = keep.tile([P, PASSES, N], I32, name="wv_raw")
         scale_raw = keep.tile([P, PASSES, N], U8, name="scale_raw")
         nc.gpsimd.memset(scale_raw[:].bitcast(I32), 0)
         bias = keep.tile([P, PACK], F32, name="bias")
@@ -69,23 +82,36 @@ def tile_list_hwayreluP_kernel(
                     scales[:, 4 * q : 4 * q + 4, :].rearrange("a r n -> r a n").bitcast(I32),
                 )
 
-        nc.sync.dma_start(wgt_sb[:, 0:HALF], wgt[:, 0:HALF])
-        nc.sync.dma_start(planes[0][0][:], x_rows[0, 0])
-        nc.sync.dma_start(wgt_sb[:, HALF:J], wgt[:, HALF:J])
-        for i in range(1, PACK):
+        for i in range(PACK):
             nc.sync.dma_start(planes[0][i][:], x_rows[0, i])
         for i in range(QUADS // 2):
             load_scales(2 * i)
             load_scales(2 * i + 1)
             nc.sync.dma_start(planes[1][i][:], x_rows[1, i])
         nc.sync.dma_start(wv_raw[:], wv_words.rearrange("a p n i -> p a (n i)").bitcast(I32))
+        nc.sync.dma_start(planes[1][2][:], x_rows[1, 2])
+        nc.sync.dma_start(planes[1][3][:], x_rows[1, 3])
         nc.sync.dma_start(bias[:], bg.rearrange("(p t) -> p t", t=PACK))
-        for i in range(QUADS // 2, PACK):
-            nc.sync.dma_start(planes[1][i][:], x_rows[1, i])
         res_rows = res.rearrange("(p t) j -> p t j", t=PACK)
         res_sb = [keep.tile([P, PACK, WIDTHS[c]], F32, name=f"res{c}") for c in range(CHUNKS)]
         for c in range(CHUNKS):
             nc.sync.dma_start(res_sb[c][:], res_rows[:, :, chunk(c)])
+
+        turned = psum.tile([P, BANK], F32, name="turned", tag="sum")
+        nc.tensor.transpose(turned[:, 0:P], wgt_rows[:], identity[:])
+        by_piece = turned[:, 0 : HEADS * PIECES].rearrange("p (g r) -> p r g", r=PIECES)
+        per_half = PIECES // 2
+        repeated = [keep.tile([P, per_half, HEADS, GROUP], F32, name=f"repeated{h}") for h in range(2)]
+        for h in range(2):
+            source = by_piece[:, h * per_half : (h + 1) * per_half, :].unsqueeze(3)
+            nc.scalar.copy(repeated[h][:], source.to_broadcast([P, per_half, HEADS, GROUP]))
+        for h in range(2):
+            back = psum.tile([P, BANK], F32, name="back", tag="sum")
+            for r in range(per_half):
+                nc.tensor.transpose(
+                    back[:, r * P : (r + 1) * P], repeated[h][:, r].rearrange("p g s -> p (g s)"), identity[:]
+                )
+            nc.scalar.copy(wgt_sb[:, h * HALF : (h + 1) * HALF], back[:])
 
         wk_dealt = keep.tile([P, PASSES, 2 * N], U8, name="wk_dealt", align_bytes=64)
         for a in range(PASSES):
@@ -114,6 +140,12 @@ def tile_list_hwayreluP_kernel(
                 src.rearrange("p t (c i) -> p c t i", i=4),
             )
 
+        def weave_pair(dst, src, u):
+            nc.scalar.copy(
+                dst.rearrange("p (c i t) -> p c t i", i=4, t=PACK)[:, :, 2 * u : 2 * u + 2, :],
+                src.rearrange("p t (c i) -> p c t i", i=4),
+            )
+
         halves = [slice(0, HALF), slice(HALF, J)]
         picked0 = keep.tile([P, PACK, J], F32, name="picked0")
         for cols in halves:
@@ -121,73 +153,77 @@ def tile_list_hwayreluP_kernel(
         for i in range(1, PACK):
             gather(picked0[:, i, :], 0, i, slice(0, J))
         woven0 = keep.tile([P, PACK * J], BF16, name="woven0", align_bytes=64)
-        for cols in halves:
-            weave(nc.scalar.copy, woven0[:, PACK * cols.start : PACK * cols.stop], picked0[:, :, cols])
-        codes0 = keep.tile([P, J], U32, name="codes0", tag="wv_then_codes", align_bytes=64)
+        for u in range(2):
+            weave_pair(woven0[:], picked0[:, 2 * u : 2 * u + 2, :], u)
+
+        picked1 = keep.tile([P, PACK, J], F32, name="picked1")
+        for i in range(2):
+            gather(picked1[:, i, :], 1, i, slice(0, J))
+        codes0 = keep.tile([P, J], U32, name="codes0", tag="x11", align_bytes=64)
         scales0 = keep.tile([P, J], U8, name="scales0", align_bytes=64)
         nc.vector.quantize_mx(codes0[:].bitcast(FP8X4), scales0[:], woven0[:])
+        woven1 = [keep.tile([P, PACK * WIDTHS[c]], BF16, name=f"woven1_{c}", align_bytes=64) for c in range(CHUNKS)]
+        for c in range(CHUNKS):
+            weave_pair(woven1[c][:], picked1[:, 0:2, chunk(c)], 0)
+        gather(picked1[:, 2, :], 1, 2, slice(0, J))
 
-        picked1 = keep.tile([P, PACK, STARTS[LAST]], F32, name="picked1")
-        for i in range(PACK - 1):
-            gather(picked1[:, i, :], 1, i, slice(0, STARTS[LAST]))
-        for c in range(LAST):
+        def gather_last_plane(c):
             gather(picked1[:, PACK - 1, chunk(c)], 1, PACK - 1, chunk(c))
+            weave_pair(woven1[c][:], picked1[:, 2:PACK, chunk(c)], 1)
 
         out_rows = out_0.rearrange("(p t) j -> p t j", t=PACK)
         out_words = out_1[0].rearrange("p j i -> p (j i)").bitcast(I32)
         y_scales = keep.tile([P, J], U8, name="y_scales", align_bytes=64)
-        picked_of = {c: picked1[:, :, chunk(c)] for c in range(LAST)}
         operand1, banks, gate, diff, step, y = {}, {}, {}, {}, {}, {}
 
         def quantise_pass1(c):
-            woven = keep.tile([P, PACK * WIDTHS[c]], BF16, name=f"woven1_{c}", tag=f"woven1_{c}", align_bytes=64)
-            weave(nc.scalar.copy, woven[:], picked_of[c])
+            woven = woven1[c]
             codes = keep.tile([P, WIDTHS[c]], U32, name=f"codes1_{c}", align_bytes=64)
             scales = keep.tile([P, WIDTHS[c]], U8, name=f"scales1_{c}", align_bytes=64)
             nc.vector.quantize_mx(codes[:].bitcast(FP8X4), scales[:], woven[:])
             operand1[c] = (codes, scales)
 
-        def gather_last_chunk():
-            picked = keep.tile([P, PACK, WIDTHS[LAST]], F32, name="picked_last", tag="woven1_0", align_bytes=64)
-            for i in range(PACK):
-                gather(picked[:, i, :], 1, i, chunk(LAST))
-            picked_of[LAST] = picked[:]
+        def open_banks(c):
+            banks[c] = [
+                (psum.tile([P, BANK], F32, name="ke", tag="sum"), psum.tile([P, BANK], F32, name="ve", tag="sum"))
+                for b in range(PACK * WIDTHS[c] // BANK)
+            ]
 
-        def multiply(c, a):
+        def moving(c, a):
+            return (codes0, scales0, STARTS[c]) if a == 0 else (operand1[c][0], operand1[c][1], 0)
+
+        def multiply_k(c, a):
             width = WIDTHS[c]
             per_bank = BANK // width
-            if a == 0:
-                banks[c] = [
-                    (psum.tile([P, BANK], F32, name="ke", tag="sum"), psum.tile([P, BANK], F32, name="ve", tag="sum"))
-                    for b in range(PACK // per_bank)
-                ]
-                codes, scales, j0 = codes0, scales0, STARTS[c]
-            else:
-                codes, scales, j0 = operand1[c][0], operand1[c][1], 0
-            for b, (ke, ve) in enumerate(banks[c]):
-                for u in range(per_bank):
-                    t = b * per_bank + u
-                    for s in range(0, width, P):
-                        nc.tensor.matmul_mx(
-                            ke[:, u * width + s : u * width + s + P],
-                            lhsT=wk_dealt[:, a, 2 * t * P : 2 * (t + 1) * P].bitcast(FP4X4),
-                            lhsT_scale=scale_dealt[:, a, t * P : (t + 1) * P],
-                            rhs=codes[:, j0 + s : j0 + s + P].bitcast(FP8X4),
-                            rhs_scale=scales[:, j0 + s : j0 + s + P],
-                            start=(a == 0 and u == 0 and s == 0),
-                            stop=(a == PASSES - 1 and u == per_bank - 1 and s == width - P),
-                        )
-                for u in range(per_bank):
-                    t = b * per_bank + u
+            codes, scales, j0 = moving(c, a)
+            for t in range(PACK):
+                b, u = divmod(t, per_bank)
+                for s in range(0, width, P):
                     nc.tensor.matmul_mx(
-                        ve[:, u * width : (u + 1) * width],
-                        lhsT=wv_dealt[:, a, t * P : (t + 1) * P].bitcast(FP8X4),
-                        lhsT_scale=scale_dealt[WV_ROW:P, a, t * P : (t + 1) * P],
-                        rhs=codes[:, j0 : j0 + width].bitcast(FP8X4),
-                        rhs_scale=scales[:, j0 : j0 + width],
-                        start=(a == 0 and u == 0),
-                        stop=(a == PASSES - 1 and u == per_bank - 1),
+                        banks[c][b][0][:, u * width + s : u * width + s + P],
+                        lhsT=wk_dealt[:, a, 2 * t * P : 2 * (t + 1) * P].bitcast(FP4X4),
+                        lhsT_scale=scale_dealt[:, a, t * P : (t + 1) * P],
+                        rhs=codes[:, j0 + s : j0 + s + P].bitcast(FP8X4),
+                        rhs_scale=scales[:, j0 + s : j0 + s + P],
+                        start=(a == 0 and u == 0 and s == 0),
+                        stop=(a == PASSES - 1 and u == per_bank - 1 and s == width - P),
                     )
+
+        def multiply_v(c, a):
+            width = WIDTHS[c]
+            per_bank = BANK // width
+            codes, scales, j0 = moving(c, a)
+            for t in range(PACK):
+                b, u = divmod(t, per_bank)
+                nc.tensor.matmul_mx(
+                    banks[c][b][1][:, u * width : (u + 1) * width],
+                    lhsT=wv_dealt[:, a, t * P : (t + 1) * P].bitcast(FP8X4),
+                    lhsT_scale=scale_dealt[WV_ROW:P, a, t * P : (t + 1) * P],
+                    rhs=codes[:, j0 : j0 + width].bitcast(FP8X4),
+                    rhs_scale=scales[:, j0 : j0 + width],
+                    start=(a == 0 and u == 0),
+                    stop=(a == PASSES - 1 and u == per_bank - 1),
+                )
 
         def read_banks(c):
             width = WIDTHS[c]
@@ -214,7 +250,7 @@ def tile_list_hwayreluP_kernel(
             return tile[:].rearrange("p t j -> p (t j)")
 
         def gpsimd_share(c):
-            return GPSIMD_SHARE if c < LAST and WIDTHS[c + 1] == max(WIDTHS) else 0
+            return GPSIMD_SHARE[WIDTHS[c + 1]] if c < LAST else 0
 
         def apply_gate(c):
             step[c] = keep.tile([P, PACK, WIDTHS[c]], F32, name=f"step{c}")
@@ -233,33 +269,61 @@ def tile_list_hwayreluP_kernel(
             nc.vector.tensor_tensor(*[ap[:, share:] for ap in operands], ALU.add)
             nc.sync.dma_start(out_rows[:, :, chunk(c)], y[c][:])
 
-        def hand_on(c):
-            y_woven = keep.tile([P, PACK * WIDTHS[c]], BF16, name=f"y_woven{c}", align_bytes=64)
-            weave(nc.vector.tensor_copy if c == LAST else nc.scalar.copy, y_woven[:], y[c][:])
-            y_codes = keep.tile([P, WIDTHS[c]], U32, name=f"y_codes{c}", align_bytes=64)
-            nc.vector.quantize_mx(y_codes[:].bitcast(FP8X4), y_scales[:, chunk(c)], y_woven[:])
-            nc.sync.dma_start(out_words[:, chunk(c)], y_codes[:].bitcast(I32))
+        def weave_y(c, copy, cols):
+            woven = keep.tile([P, PACK * (cols.stop - cols.start)], BF16, name=f"y_woven{c}_{cols.start}", align_bytes=64)
+            weave(copy, woven[:], y[c][:, :, cols])
+            return woven
 
+        def quantise_y(c, woven, cols):
+            y_codes = y_words[c][:, cols]
+            scales = y_scales[:, STARTS[c] + cols.start : STARTS[c] + cols.stop]
+            nc.vector.quantize_mx(y_codes.bitcast(FP8X4), scales, woven[:])
+
+        def store_words(c):
+            nc.sync.dma_start(out_words[:, chunk(c)], y_words[c][:].bitcast(I32))
+
+        def hand_on(c):
+            whole = slice(0, WIDTHS[c])
+            quantise_y(c, weave_y(c, nc.scalar.copy, whole), whole)
+            store_words(c)
+
+        y_words = [keep.tile([P, WIDTHS[c]], U32, name=f"y_words{c}", align_bytes=64) for c in range(CHUNKS)]
         for c in range(EARLY):
-            multiply(c, 0)
-        quantise_pass1(0)
-        gather_last_chunk()
-        for c in range(1, AHEAD):
+            open_banks(c)
+            multiply_k(c, 0)
+            multiply_v(c, 0)
+        gather_last_plane(0)
+        gather_last_plane(1)
+        for c in range(AHEAD):
             quantise_pass1(c)
-        for c in range(CHUNKS + 2):
-            if c < CHUNKS:
-                if c >= EARLY:
-                    multiply(c, 0)
-                multiply(c, 1)
-                read_banks(c)
+            gather_last_plane(c + 2)
+        for c in range(CHUNKS):
+            if c >= EARLY:
+                open_banks(c)
+                multiply_k(c, 0)
+                multiply_v(c, 0)
+            multiply_k(c, 1)
+            multiply_v(c, 1)
+            read_banks(c)
+            if c + AHEAD + 2 < CHUNKS:
+                gather_last_plane(c + AHEAD + 2)
             if c + AHEAD < CHUNKS:
                 quantise_pass1(c + AHEAD)
+            if c >= 1:
+                add_res(c - 1)
+            if c == LAST:
+                apply_gate(c)
             if c >= 2:
                 hand_on(c - 2)
-            if 1 <= c <= CHUNKS:
-                add_res(c - 1)
-            if c < CHUNKS:
+            if c < LAST:
                 apply_gate(c)
+        add_res(LAST)
+        hand_on(LAST - 1)
+        parts = [slice(0, WIDTHS[LAST] // 2), slice(WIDTHS[LAST] // 2, WIDTHS[LAST])]
+        woven_parts = [weave_y(LAST, nc.vector.tensor_copy, cols) for cols in parts]
+        for cols, woven in zip(parts, woven_parts):
+            quantise_y(LAST, woven, cols)
+        store_words(LAST)
         for q in range(QUADS):
             queue = nc.scalar if q % 2 else nc.sync
             queue.dma_start(out_2[0, 4 * q : 4 * q + 4, :].bitcast(I32), y_scales[32 * q : 32 * q + 4, :].bitcast(I32))

@@ -22,8 +22,10 @@ PACK = 4
 PASSES = K // (P * PACK)
 GROUP = 16
 QUADS = 4
+ROWS = 16
 WV_ROW = 4
 HALF = J // 2
+FIRST_CUTS = [slice(0, J // 4), slice(J // 4, HALF), slice(HALF, J)]
 HEADS = P // GROUP
 PIECES = J // P
 BANK = 512
@@ -49,7 +51,7 @@ def tile_list_hwayreluP_kernel(
             return slice(STARTS[c], STARTS[c] + WIDTHS[c])
 
         wgt_rows = keep.tile([P, P], F32, name="wgt_rows")
-        nc.gpsimd.memset(wgt_rows[HEADS * PIECES : P, :], 0.0)
+        nc.vector.memset(wgt_rows[HEADS * PIECES : P, :], 0.0)
         nc.sync.dma_start(
             wgt_rows[0 : HEADS * PIECES, :], wgt.rearrange("(g s) (r c) -> s g r c", s=GROUP, r=PIECES)[0]
         )
@@ -66,20 +68,30 @@ def tile_list_hwayreluP_kernel(
             for a in range(PASSES)
         ]
         wgt_sb = keep.tile([P, J], F32, name="wgt_sb")
-        wv_raw = keep.tile([P, PASSES, N], I32, name="wv_raw")
+        wv_raw = [keep.tile([P, N], I32, name=f"wv_raw{a}") for a in range(PASSES)]
         scale_raw = keep.tile([P, PASSES, N], U8, name="scale_raw")
-        nc.gpsimd.memset(scale_raw[:].bitcast(I32), 0)
+        for rows in (slice(32, 64), slice(64, P)):
+            nc.gpsimd.memset(scale_raw[rows].bitcast(I32), 0)
+        for s, scales in enumerate((wk_scales, wv_scales)):
+            nc.sync.dma_start(
+                scale_raw[ROWS * s : ROWS * (s + 1)].bitcast(I32), scales.rearrange("a q n -> q a n").bitcast(I32)
+            )
+        scale_rows = keep.tile([P, PASSES, N], U8, name="scale_rows")
+        nc.vector.tensor_copy(
+            scale_rows[:].rearrange("p a (t mb mi) -> p a mb t mi", t=PACK, mi=16),
+            scale_raw[:].rearrange("p a (mb mi t) -> p a mb t mi", t=PACK, mi=16),
+        )
+        scale_dealt = keep.tile([P, PASSES, N], U8, name="scale_dealt", align_bytes=64)
+        nc.gpsimd.memset(scale_dealt[:].bitcast(I32), 0)
         bias = keep.tile([P, PACK], F32, name="bias")
-        warm_in = keep.tile([P, 8], F32, name="warm_in")
-        nc.gpsimd.memset(warm_in[:], 0.0)
         warm_out = keep.tile([P, 8], F32, name="warm_out")
-        nc.scalar.activation(warm_out[:], warm_in[:], ACT.Sigmoid)
+        nc.scalar.activation(warm_out[HEADS * PIECES : P, :], wgt_rows[HEADS * PIECES : P, 0:8], ACT.Sigmoid)
 
         def load_scales(q):
-            for row0, scales in ((0, wk_scales), (WV_ROW, wv_scales)):
+            for s, row0 in enumerate((0, WV_ROW)):
                 nc.sync.dma_start(
-                    scale_raw[32 * q + row0 : 32 * q + row0 + 4].bitcast(I32),
-                    scales[:, 4 * q : 4 * q + 4, :].rearrange("a r n -> r a n").bitcast(I32),
+                    scale_dealt[32 * q + row0 : 32 * q + row0 + 4].bitcast(I32),
+                    scale_rows[ROWS * s + 4 * q : ROWS * s + 4 * q + 4].bitcast(I32),
                 )
 
         for i in range(PACK):
@@ -88,9 +100,11 @@ def tile_list_hwayreluP_kernel(
             load_scales(2 * i)
             load_scales(2 * i + 1)
             nc.sync.dma_start(planes[1][i][:], x_rows[1, i])
-        nc.sync.dma_start(wv_raw[:], wv_words.rearrange("a p n i -> p a (n i)").bitcast(I32))
+        wv_rows = wv_words.rearrange("a p n i -> a p (n i)").bitcast(I32)
+        nc.sync.dma_start(wv_raw[0][:], wv_rows[0])
         nc.sync.dma_start(planes[1][2][:], x_rows[1, 2])
         nc.sync.dma_start(planes[1][3][:], x_rows[1, 3])
+        nc.sync.dma_start(wv_raw[1][:], wv_rows[1])
         nc.sync.dma_start(bias[:], bg.rearrange("(p t) -> p t", t=PACK))
         res_rows = res.rearrange("(p t) j -> p t j", t=PACK)
         res_sb = [keep.tile([P, PACK, WIDTHS[c]], F32, name=f"res{c}") for c in range(CHUNKS)]
@@ -100,18 +114,19 @@ def tile_list_hwayreluP_kernel(
         turned = psum.tile([P, BANK], F32, name="turned", tag="sum")
         nc.tensor.transpose(turned[:, 0:P], wgt_rows[:], identity[:])
         by_piece = turned[:, 0 : HEADS * PIECES].rearrange("p (g r) -> p r g", r=PIECES)
-        per_half = PIECES // 2
-        repeated = [keep.tile([P, per_half, HEADS, GROUP], F32, name=f"repeated{h}") for h in range(2)]
-        for h in range(2):
-            source = by_piece[:, h * per_half : (h + 1) * per_half, :].unsqueeze(3)
-            nc.scalar.copy(repeated[h][:], source.to_broadcast([P, per_half, HEADS, GROUP]))
-        for h in range(2):
+        repeated = []
+        for cols in FIRST_CUTS:
+            count = (cols.stop - cols.start) // P
+            wide = keep.tile([P, count, HEADS, GROUP], F32, name=f"repeated{cols.start}")
+            source = by_piece[:, cols.start // P : cols.stop // P, :].unsqueeze(3)
+            nc.scalar.copy(wide[:], source.to_broadcast([P, count, HEADS, GROUP]))
+            repeated.append(wide)
+        for cols, wide in zip(FIRST_CUTS, repeated):
+            width = cols.stop - cols.start
             back = psum.tile([P, BANK], F32, name="back", tag="sum")
-            for r in range(per_half):
-                nc.tensor.transpose(
-                    back[:, r * P : (r + 1) * P], repeated[h][:, r].rearrange("p g s -> p (g s)"), identity[:]
-                )
-            nc.scalar.copy(wgt_sb[:, h * HALF : (h + 1) * HALF], back[:])
+            for r in range(width // P):
+                nc.tensor.transpose(back[:, r * P : (r + 1) * P], wide[:, r].rearrange("p g s -> p (g s)"), identity[:])
+            nc.scalar.copy(wgt_sb[:, cols], back[:, 0:width])
 
         wk_dealt = keep.tile([P, PASSES, 2 * N], U8, name="wk_dealt", align_bytes=64)
         for a in range(PASSES):
@@ -119,16 +134,12 @@ def tile_list_hwayreluP_kernel(
                 wk_dealt[:, a, :].rearrange("p (t mb mi b) -> p mb t mi b", t=PACK, mi=8, b=2),
                 wk_raw[:, a, :].rearrange("p (mb mi t b) -> p mb t mi b", t=PACK, mi=8, b=2),
             )
-        wv_dealt = keep.tile([P, PASSES, N], I32, name="wv_dealt", align_bytes=64)
-        nc.vector.tensor_copy(
-            wv_dealt[:].rearrange("p a (t mb mi) -> p a mb t mi", t=PACK, mi=4),
-            wv_raw[:].rearrange("p a (mb mi t) -> p a mb t mi", t=PACK, mi=4),
-        )
-        scale_dealt = keep.tile([P, PASSES, N], U8, name="scale_dealt", align_bytes=64)
-        nc.vector.tensor_copy(
-            scale_dealt[:].rearrange("p a (t mb mi) -> p a mb t mi", t=PACK, mi=16),
-            scale_raw[:].rearrange("p a (mb mi t) -> p a mb t mi", t=PACK, mi=16),
-        )
+        wv_dealt = [keep.tile([P, N], I32, name=f"wv_dealt{a}", align_bytes=64) for a in range(PASSES)]
+        for a in range(PASSES):
+            nc.vector.tensor_copy(
+                wv_dealt[a][:].rearrange("p (t mb mi) -> p mb t mi", t=PACK, mi=4),
+                wv_raw[a][:].rearrange("p (mb mi t) -> p mb t mi", t=PACK, mi=4),
+            )
 
         def gather(dst, a, i, cols):
             picks = offsets[:, cols.start // GROUP : cols.stop // GROUP]
@@ -146,9 +157,8 @@ def tile_list_hwayreluP_kernel(
                 src.rearrange("p t (c i) -> p c t i", i=4),
             )
 
-        halves = [slice(0, HALF), slice(HALF, J)]
         picked0 = keep.tile([P, PACK, J], F32, name="picked0")
-        for cols in halves:
+        for cols in FIRST_CUTS:
             gather(picked0[:, 0, cols], 0, 0, cols)
         for i in range(1, PACK):
             gather(picked0[:, i, :], 0, i, slice(0, J))
@@ -217,7 +227,7 @@ def tile_list_hwayreluP_kernel(
                 b, u = divmod(t, per_bank)
                 nc.tensor.matmul_mx(
                     banks[c][b][1][:, u * width : (u + 1) * width],
-                    lhsT=wv_dealt[:, a, t * P : (t + 1) * P].bitcast(FP8X4),
+                    lhsT=wv_dealt[a][:, t * P : (t + 1) * P].bitcast(FP8X4),
                     lhsT_scale=scale_dealt[WV_ROW:P, a, t * P : (t + 1) * P],
                     rhs=codes[:, j0 : j0 + width].bitcast(FP8X4),
                     rhs_scale=scales[:, j0 : j0 + width],

@@ -37,6 +37,7 @@ LAST = CHUNKS - 1
 EARLY = 2
 AHEAD = 2
 GPSIMD_SHARE = {256: 384, 128: 128}
+HELD = 1
 
 
 def tile_list_hwayreluP_kernel(
@@ -84,6 +85,7 @@ def tile_list_hwayreluP_kernel(
         scale_dealt = keep.tile([P, PASSES, N], U8, name="scale_dealt", align_bytes=64)
         nc.gpsimd.memset(scale_dealt[:].bitcast(I32), 0)
         bias = keep.tile([P, PACK], F32, name="bias")
+        neg_bias = keep.tile([P, PACK], F32, name="neg_bias")
         warm_out = keep.tile([P, 8], F32, name="warm_out")
         nc.scalar.activation(warm_out[HEADS * PIECES : P, :], wgt_rows[HEADS * PIECES : P, 0:8], ACT.Sigmoid)
 
@@ -106,6 +108,7 @@ def tile_list_hwayreluP_kernel(
         nc.sync.dma_start(planes[1][3][:], x_rows[1, 3])
         nc.sync.dma_start(wv_raw[1][:], wv_rows[1])
         nc.sync.dma_start(bias[:], bg.rearrange("(p t) -> p t", t=PACK))
+        nc.scalar.mul(neg_bias[:], bias[:], -1.0)
         res_rows = res.rearrange("(p t) j -> p t j", t=PACK)
         res_sb = [keep.tile([P, PACK, WIDTHS[c]], F32, name=f"res{c}") for c in range(CHUNKS)]
         for c in range(CHUNKS):
@@ -194,10 +197,16 @@ def tile_list_hwayreluP_kernel(
             operand1[c] = (codes, scales)
 
         def open_banks(c):
-            banks[c] = [
-                (psum.tile([P, BANK], F32, name="ke", tag="sum"), psum.tile([P, BANK], F32, name="ve", tag="sum"))
-                for b in range(PACK * WIDTHS[c] // BANK)
-            ]
+            count = PACK * WIDTHS[c] // BANK
+            if c == 2:
+                ke = [psum.tile([P, BANK], F32, name="ke", tag="sum") for b in range(count)]
+                ve = [psum.tile([P, BANK], F32, name="ve", tag="sum") for b in range(count)]
+                banks[c] = list(zip(ke, ve))
+            else:
+                banks[c] = [
+                    (psum.tile([P, BANK], F32, name="ke", tag="sum"), psum.tile([P, BANK], F32, name="ve", tag="sum"))
+                    for b in range(count)
+                ]
 
         def moving(c, a):
             return (codes0, scales0, STARTS[c]) if a == 0 else (operand1[c][0], operand1[c][1], 0)
@@ -219,12 +228,12 @@ def tile_list_hwayreluP_kernel(
                         stop=(a == PASSES - 1 and u == per_bank - 1 and s == width - P),
                     )
 
-        def multiply_v(c, a):
+        def multiply_v(c, a, b):
             width = WIDTHS[c]
             per_bank = BANK // width
             codes, scales, j0 = moving(c, a)
-            for t in range(PACK):
-                b, u = divmod(t, per_bank)
+            for u in range(per_bank):
+                t = b * per_bank + u
                 nc.tensor.matmul_mx(
                     banks[c][b][1][:, u * width : (u + 1) * width],
                     lhsT=wv_dealt[a][:, t * P : (t + 1) * P].bitcast(FP8X4),
@@ -243,9 +252,11 @@ def tile_list_hwayreluP_kernel(
             for b, (ke, ve) in enumerate(banks[c]):
                 for u in range(per_bank):
                     t = b * per_bank + u
-                    nc.scalar.activation(
-                        gate[c][:, t, :], ke[:, u * width : (u + 1) * width], ACT.Sigmoid, bias=bias[:, t : t + 1]
-                    )
+                    sums = ke[:, u * width : (u + 1) * width]
+                    if c < HELD:
+                        nc.scalar.activation(gate[c][:, t, :], sums, ACT.Sigmoid, bias=bias[:, t : t + 1])
+                    else:
+                        nc.scalar.activation(gate[c][:, t, :], sums, ACT.Sigmoid, bias=neg_bias[:, t : t + 1], scale=-1.0)
                 rows = slice(b * per_bank, (b + 1) * per_bank)
                 nc.vector.scalar_tensor_tensor(
                     diff[c][:, rows, :].rearrange("p t j -> p (t j)"),
@@ -280,7 +291,8 @@ def tile_list_hwayreluP_kernel(
             nc.sync.dma_start(out_rows[:, :, chunk(c)], y[c][:])
 
         def weave_y(c, copy, cols):
-            woven = keep.tile([P, PACK * (cols.stop - cols.start)], BF16, name=f"y_woven{c}_{cols.start}", align_bytes=64)
+            name = f"y_woven{c}_{cols.start}"
+            woven = keep.tile([P, PACK * (cols.stop - cols.start)], BF16, name=name, tag=name, align_bytes=64)
             weave(copy, woven[:], y[c][:, :, cols])
             return woven
 
@@ -301,34 +313,82 @@ def tile_list_hwayreluP_kernel(
         for c in range(EARLY):
             open_banks(c)
             multiply_k(c, 0)
-            multiply_v(c, 0)
+            for b in range(len(banks[c])):
+                multiply_v(c, 0, b)
         gather_last_plane(0)
         gather_last_plane(1)
         for c in range(AHEAD):
             quantise_pass1(c)
             gather_last_plane(c + 2)
-        for c in range(CHUNKS):
+        def sums(c):
             if c >= EARLY:
                 open_banks(c)
                 multiply_k(c, 0)
-                multiply_v(c, 0)
             multiply_k(c, 1)
-            multiply_v(c, 1)
+            for b in range(len(banks[c])):
+                if c >= EARLY:
+                    multiply_v(c, 0, b)
+                multiply_v(c, 1, b)
             read_banks(c)
-            if c + AHEAD + 2 < CHUNKS:
-                gather_last_plane(c + AHEAD + 2)
-            if c + AHEAD < CHUNKS:
-                quantise_pass1(c + AHEAD)
-            if c >= 1:
-                add_res(c - 1)
-            if c == LAST:
-                apply_gate(c)
-            if c >= 2:
-                hand_on(c - 2)
-            if c < LAST:
-                apply_gate(c)
-        add_res(LAST)
-        hand_on(LAST - 1)
+
+        def product(engine, dst, c, span):
+            engine.tensor_tensor(dst, flat(diff[c])[:, span], flat(gate[c])[:, span], ALU.mult)
+
+        def finish(c, span, made):
+            b = span.start // BANK
+            ve = banks[c][b][1][:, span.start - b * BANK : span.stop - b * BANK]
+            nc.vector.scalar_tensor_tensor(flat(y[c])[:, span], ve, 0.0, made, ALU.max, ALU.subtract)
+
+        for c in range(HELD, CHUNKS):
+            y[c] = keep.tile([P, PACK, WIDTHS[c]], F32, name=f"y{c}")
+            step[c] = keep.tile([P, PACK, WIDTHS[c]], F32, name=f"step{c}")
+
+        sums(0)
+        gather_last_plane(4)
+        quantise_pass1(2)
+        apply_gate(0)
+
+        sums(1)
+        quantise_pass1(3)
+        add_res(0)
+        low, high = slice(0, BANK), slice(BANK, 2 * BANK)
+        made1 = flat(step[0])
+        product(nc.gpsimd, made1, 1, high)
+        product(nc.vector, flat(step[1])[:, low], 1, low)
+
+        sums(2)
+        finish(1, low, flat(step[1])[:, low])
+        product(nc.gpsimd, flat(step[2])[:, 0:256], 2, slice(0, 256))
+        finish(1, high, made1)
+        nc.sync.dma_start(out_rows[:, :, chunk(1)], y[1][:])
+        quantise_pass1(4)
+        hand_on(0)
+        made2_tile = keep.tile([P, BANK], F32, name="made2", tag="y_woven0_0", align_bytes=64)
+        made2 = made2_tile[:]
+        product(nc.gpsimd, made2, 2, high)
+        product(nc.vector, flat(step[2])[:, 256:BANK], 2, slice(256, BANK))
+
+        sums(3)
+        finish(2, low, flat(step[2])[:, low])
+        product(nc.gpsimd, flat(step[3])[:, 0:256], 3, slice(0, 256))
+        finish(2, high, made2)
+        nc.sync.dma_start(out_rows[:, :, chunk(2)], y[2][:])
+        hand_on(1)
+        made3 = keep.tile([P, 384], F32, name="made3", tag="y_woven1_0", align_bytes=64)
+        product(nc.gpsimd, made3[:], 3, slice(640, 1024))
+        product(nc.vector, flat(step[3])[:, 256:640], 3, slice(256, 640))
+
+        sums(4)
+        finish(3, slice(0, BANK), flat(step[3])[:, 0:BANK])
+        finish(3, slice(BANK, 640), flat(step[3])[:, BANK:640])
+        product(nc.gpsimd, flat(step[4])[:, 0:128], 4, slice(0, 128))
+        finish(3, slice(640, 1024), made3[:])
+        nc.sync.dma_start(out_rows[:, :, chunk(3)], y[3][:])
+        product(nc.vector, flat(step[4])[:, 128:BANK], 4, slice(128, BANK))
+        hand_on(2)
+        finish(4, low, flat(step[4]))
+        nc.sync.dma_start(out_rows[:, :, chunk(4)], y[4][:])
+        hand_on(3)
         parts = [slice(0, WIDTHS[LAST] // 2), slice(WIDTHS[LAST] // 2, WIDTHS[LAST])]
         woven_parts = [weave_y(LAST, nc.vector.tensor_copy, cols) for cols in parts]
         for cols, woven in zip(parts, woven_parts):

@@ -36,8 +36,8 @@ CHUNKS = len(WIDTHS)
 LAST = CHUNKS - 1
 EARLY = 2
 AHEAD = 2
-GPSIMD_SHARE = {256: 384, 128: 128}
-HELD = 1
+GPSIMD_FIRST = {128: 192, 256: 320}
+GPSIMD_LAST = {128: 384, 256: 512}
 
 
 def tile_list_hwayreluP_kernel(
@@ -175,7 +175,10 @@ def tile_list_hwayreluP_kernel(
         codes0 = keep.tile([P, J], U32, name="codes0", tag="x11", align_bytes=64)
         scales0 = keep.tile([P, J], U8, name="scales0", align_bytes=64)
         nc.vector.quantize_mx(codes0[:].bitcast(FP8X4), scales0[:], woven0[:])
-        woven1 = [keep.tile([P, PACK * WIDTHS[c]], BF16, name=f"woven1_{c}", align_bytes=64) for c in range(CHUNKS)]
+        woven1 = [
+            keep.tile([P, PACK * WIDTHS[c]], BF16, name=f"woven1_{c}", tag=f"woven1_{c}", align_bytes=64)
+            for c in range(CHUNKS)
+        ]
         for c in range(CHUNKS):
             weave_pair(woven1[c][:], picked1[:, 0:2, chunk(c)], 0)
         gather(picked1[:, 2, :], 1, 2, slice(0, J))
@@ -253,10 +256,7 @@ def tile_list_hwayreluP_kernel(
                 for u in range(per_bank):
                     t = b * per_bank + u
                     sums = ke[:, u * width : (u + 1) * width]
-                    if c < HELD:
-                        nc.scalar.activation(gate[c][:, t, :], sums, ACT.Sigmoid, bias=bias[:, t : t + 1])
-                    else:
-                        nc.scalar.activation(gate[c][:, t, :], sums, ACT.Sigmoid, bias=neg_bias[:, t : t + 1], scale=-1.0)
+                    nc.scalar.activation(gate[c][:, t, :], sums, ACT.Sigmoid, bias=neg_bias[:, t : t + 1], scale=-1.0)
                 rows = slice(b * per_bank, (b + 1) * per_bank)
                 nc.vector.scalar_tensor_tensor(
                     diff[c][:, rows, :].rearrange("p t j -> p (t j)"),
@@ -269,26 +269,6 @@ def tile_list_hwayreluP_kernel(
 
         def flat(tile):
             return tile[:].rearrange("p t j -> p (t j)")
-
-        def gpsimd_share(c):
-            return GPSIMD_SHARE[WIDTHS[c + 1]] if c < LAST else 0
-
-        def apply_gate(c):
-            step[c] = keep.tile([P, PACK, WIDTHS[c]], F32, name=f"step{c}")
-            operands = [flat(step[c]), flat(diff[c]), flat(gate[c])]
-            share = gpsimd_share(c)
-            if share:
-                nc.vector.tensor_tensor(*[ap[:, :share] for ap in operands], ALU.mult)
-            nc.vector.tensor_tensor(*[ap[:, share:] for ap in operands], ALU.mult)
-
-        def add_res(c):
-            y[c] = keep.tile([P, PACK, WIDTHS[c]], F32, name=f"y{c}")
-            operands = [flat(y[c]), flat(step[c]), flat(res_sb[c])]
-            share = gpsimd_share(c)
-            if share:
-                nc.gpsimd.tensor_tensor(*[ap[:, :share] for ap in operands], ALU.add)
-            nc.vector.tensor_tensor(*[ap[:, share:] for ap in operands], ALU.add)
-            nc.sync.dma_start(out_rows[:, :, chunk(c)], y[c][:])
 
         def weave_y(c, copy, cols):
             name = f"y_woven{c}_{cols.start}"
@@ -339,58 +319,47 @@ def tile_list_hwayreluP_kernel(
             ve = banks[c][b][1][:, span.start - b * BANK : span.stop - b * BANK]
             nc.vector.scalar_tensor_tensor(flat(y[c])[:, span], ve, 0.0, made, ALU.max, ALU.subtract)
 
-        for c in range(HELD, CHUNKS):
+        def first_share(c):
+            return GPSIMD_FIRST[min(WIDTHS[c - 1], WIDTHS[c])] if c > 0 else 0
+
+        def last_start(c):
+            return PACK * WIDTHS[c] - (GPSIMD_LAST[min(WIDTHS[c], WIDTHS[c + 1])] if c < LAST else 0)
+
+        def finish_span(c, start, stop, made):
+            for lo in range(start - start % BANK, stop, BANK):
+                span = slice(max(lo, start), min(lo + BANK, stop))
+                finish(c, span, made[:, span.start - start : span.stop - start])
+                if span.stop % BANK == 0:
+                    rows = slice((span.stop - BANK) // WIDTHS[c], span.stop // WIDTHS[c])
+                    nc.sync.dma_start(out_rows[:, rows, chunk(c)], y[c][:, rows, :])
+
+        late = {}
+        for c in range(CHUNKS):
+            sums(c)
             y[c] = keep.tile([P, PACK, WIDTHS[c]], F32, name=f"y{c}")
-            step[c] = keep.tile([P, PACK, WIDTHS[c]], F32, name=f"step{c}")
-
-        sums(0)
-        gather_last_plane(4)
-        quantise_pass1(2)
-        apply_gate(0)
-
-        sums(1)
-        quantise_pass1(3)
-        add_res(0)
-        low, high = slice(0, BANK), slice(BANK, 2 * BANK)
-        made1 = flat(step[0])
-        product(nc.gpsimd, made1, 1, high)
-        product(nc.vector, flat(step[1])[:, low], 1, low)
-
-        sums(2)
-        finish(1, low, flat(step[1])[:, low])
-        product(nc.gpsimd, flat(step[2])[:, 0:256], 2, slice(0, 256))
-        finish(1, high, made1)
-        nc.sync.dma_start(out_rows[:, :, chunk(1)], y[1][:])
-        quantise_pass1(4)
-        hand_on(0)
-        made2_tile = keep.tile([P, BANK], F32, name="made2", tag="y_woven0_0", align_bytes=64)
-        made2 = made2_tile[:]
-        product(nc.gpsimd, made2, 2, high)
-        product(nc.vector, flat(step[2])[:, 256:BANK], 2, slice(256, BANK))
-
-        sums(3)
-        finish(2, low, flat(step[2])[:, low])
-        product(nc.gpsimd, flat(step[3])[:, 0:256], 3, slice(0, 256))
-        finish(2, high, made2)
-        nc.sync.dma_start(out_rows[:, :, chunk(2)], y[2][:])
-        hand_on(1)
-        made3 = keep.tile([P, 384], F32, name="made3", tag="y_woven1_0", align_bytes=64)
-        product(nc.gpsimd, made3[:], 3, slice(640, 1024))
-        product(nc.vector, flat(step[3])[:, 256:640], 3, slice(256, 640))
-
-        sums(4)
-        finish(3, slice(0, BANK), flat(step[3])[:, 0:BANK])
-        finish(3, slice(BANK, 640), flat(step[3])[:, BANK:640])
-        product(nc.gpsimd, flat(step[4])[:, 0:128], 4, slice(0, 128))
-        finish(3, slice(640, 1024), made3[:])
-        nc.sync.dma_start(out_rows[:, :, chunk(3)], y[3][:])
-        product(nc.vector, flat(step[4])[:, 128:BANK], 4, slice(128, BANK))
-        hand_on(2)
-        finish(4, low, flat(step[4]))
-        nc.sync.dma_start(out_rows[:, :, chunk(4)], y[4][:])
-        hand_on(3)
+            step[c] = keep.tile([P, last_start(c)], F32, name=f"step{c}")
+            if c >= 1:
+                finish_span(c - 1, 0, last_start(c - 1), step[c - 1][:])
+                product(nc.gpsimd, step[c][:, : first_share(c)], c, slice(0, first_share(c)))
+                finish_span(c - 1, last_start(c - 1), PACK * WIDTHS[c - 1], late[c - 1][:])
+            if c + AHEAD + 2 < CHUNKS:
+                gather_last_plane(c + AHEAD + 2)
+            if c + AHEAD < CHUNKS:
+                quantise_pass1(c + AHEAD)
+            if c < LAST:
+                if c >= 2:
+                    hand_on(c - 2)
+                behind = f"y_woven{c - 2}_0" if c >= 2 else f"woven1_{c + AHEAD}"
+                span = slice(last_start(c), PACK * WIDTHS[c])
+                late[c] = keep.tile([P, span.stop - span.start], F32, name=f"late{c}", tag=behind, align_bytes=64)
+                product(nc.gpsimd, late[c][:], c, span)
+            span = slice(first_share(c), last_start(c))
+            product(nc.vector, step[c][:, span], c, span)
+        hand_on(LAST - 2)
+        finish_span(LAST, 0, last_start(LAST), step[LAST][:])
+        hand_on(LAST - 1)
         parts = [slice(0, WIDTHS[LAST] // 2), slice(WIDTHS[LAST] // 2, WIDTHS[LAST])]
-        woven_parts = [weave_y(LAST, nc.vector.tensor_copy, cols) for cols in parts]
+        woven_parts = [weave_y(LAST, copy, cols) for copy, cols in zip((nc.scalar.copy, nc.vector.tensor_copy), parts)]
         for cols, woven in zip(parts, woven_parts):
             quantise_y(LAST, woven, cols)
         store_words(LAST)

@@ -47,6 +47,7 @@ def tile_list_hwayreluP_kernel(
     with ExitStack() as ctx:
         keep = ctx.enter_context(tc.tile_pool(name="keep", bufs=1))
         psum = ctx.enter_context(tc.psum_pool(name="psum", bufs=BANKS))
+        placed = ctx.enter_context(tc.tile_pool(name="placed", bufs=1))
 
         def chunk(c):
             return slice(STARTS[c], STARTS[c] + WIDTHS[c])
@@ -175,10 +176,30 @@ def tile_list_hwayreluP_kernel(
         codes0 = keep.tile([P, J], U32, name="codes0", tag="x11", align_bytes=64)
         scales0 = keep.tile([P, J], U8, name="scales0", align_bytes=64)
         nc.vector.quantize_mx(codes0[:].bitcast(FP8X4), scales0[:], woven0[:])
-        woven1 = [
-            keep.tile([P, PACK * WIDTHS[c]], BF16, name=f"woven1_{c}", tag=f"woven1_{c}", align_bytes=64)
-            for c in range(CHUNKS)
-        ]
+
+        def first_share(c):
+            return GPSIMD_FIRST[min(WIDTHS[c - 1], WIDTHS[c])] if c > 0 else 0
+
+        def last_start(c):
+            return PACK * WIDTHS[c] - (GPSIMD_LAST[min(WIDTHS[c], WIDTHS[c + 1])] if c < LAST else 0)
+
+        quantised = [[("xg", 2), ("xg", 3)], [("xg", 4)], [("y", 0)], [("y", 1)]]
+        input_at, late_at = {}, {}
+        free = late_end = 0
+        for c, inputs in enumerate(quantised):
+            free = max(free, late_end)
+            for kind, b in inputs:
+                input_at[kind, b] = free
+                free = free + 2 * PACK * WIDTHS[b]
+            late_at[c] = (late_end if c else input_at[inputs[-1]]) - 64
+            late_end = late_at[c] + 4 * (PACK * WIDTHS[c] - last_start(c))
+
+        def woven_tile(kind, c, width, name):
+            if (kind, c) in input_at:
+                return placed.tile([P, PACK * width], BF16, name=name, offset=input_at[kind, c], align_bytes=64)
+            return keep.tile([P, PACK * width], BF16, name=name, align_bytes=64)
+
+        woven1 = [woven_tile("xg", c, WIDTHS[c], f"woven1_{c}") for c in range(CHUNKS)]
         for c in range(CHUNKS):
             weave_pair(woven1[c][:], picked1[:, 0:2, chunk(c)], 0)
         gather(picked1[:, 2, :], 1, 2, slice(0, J))
@@ -271,8 +292,7 @@ def tile_list_hwayreluP_kernel(
             return tile[:].rearrange("p t j -> p (t j)")
 
         def weave_y(c, copy, cols):
-            name = f"y_woven{c}_{cols.start}"
-            woven = keep.tile([P, PACK * (cols.stop - cols.start)], BF16, name=name, tag=name, align_bytes=64)
+            woven = woven_tile("y", c, cols.stop - cols.start, f"y_woven{c}_{cols.start}")
             weave(copy, woven[:], y[c][:, :, cols])
             return woven
 
@@ -319,12 +339,6 @@ def tile_list_hwayreluP_kernel(
             ve = banks[c][b][1][:, span.start - b * BANK : span.stop - b * BANK]
             nc.vector.scalar_tensor_tensor(flat(y[c])[:, span], ve, 0.0, made, ALU.max, ALU.subtract)
 
-        def first_share(c):
-            return GPSIMD_FIRST[min(WIDTHS[c - 1], WIDTHS[c])] if c > 0 else 0
-
-        def last_start(c):
-            return PACK * WIDTHS[c] - (GPSIMD_LAST[min(WIDTHS[c], WIDTHS[c + 1])] if c < LAST else 0)
-
         def finish_span(c, start, stop, made):
             for lo in range(start - start % BANK, stop, BANK):
                 span = slice(max(lo, start), min(lo + BANK, stop))
@@ -344,14 +358,14 @@ def tile_list_hwayreluP_kernel(
                 finish_span(c - 1, last_start(c - 1), PACK * WIDTHS[c - 1], late[c - 1][:])
             if c + AHEAD + 2 < CHUNKS:
                 gather_last_plane(c + AHEAD + 2)
-            if c + AHEAD < CHUNKS:
-                quantise_pass1(c + AHEAD)
             if c < LAST:
-                if c >= 2:
-                    hand_on(c - 2)
-                behind = f"y_woven{c - 2}_0" if c >= 2 else f"woven1_{c + AHEAD}"
+                for kind, b in quantised[c]:
+                    if kind == "xg":
+                        quantise_pass1(b)
+                    else:
+                        hand_on(b)
                 span = slice(last_start(c), PACK * WIDTHS[c])
-                late[c] = keep.tile([P, span.stop - span.start], F32, name=f"late{c}", tag=behind, align_bytes=64)
+                late[c] = placed.tile([P, span.stop - span.start], F32, name=f"late{c}", offset=late_at[c], align_bytes=64)
                 product(nc.gpsimd, late[c][:], c, span)
             span = slice(first_share(c), last_start(c))
             product(nc.vector, step[c][:, span], c, span)

@@ -60,9 +60,9 @@ def tile_list_hwayreluP_kernel(
         identity = keep.tile([P, P], F32, name="identity")
         make_identity(nc, identity[:])
         offsets = keep.tile([P, J // GROUP], U16, name="offsets")
-        nc.sync.dma_start(offsets[:], offs)
-        wk_raw = keep.tile([P, PASSES, 2 * N], U8, name="wk_raw")
+        wk_raw = keep.tile([P, PASSES, N], U16, name="wk_raw")
         nc.sync.dma_start(wk_raw[:].bitcast(I32), wk_words.rearrange("a p b -> p a b").bitcast(I32))
+        nc.sync.dma_start(offsets[:], offs)
 
         x_rows = xT.rearrange("(a p i) t -> a i p t", a=PASSES, i=PACK)
         planes = [
@@ -132,12 +132,11 @@ def tile_list_hwayreluP_kernel(
                 nc.tensor.transpose(back[:, r * P : (r + 1) * P], wide[:, r].rearrange("p g s -> p (g s)"), identity[:])
             nc.scalar.copy(wgt_sb[:, cols], back[:, 0:width])
 
-        wk_dealt = keep.tile([P, PASSES, 2 * N], U8, name="wk_dealt", align_bytes=64)
-        for a in range(PASSES):
-            nc.vector.tensor_copy(
-                wk_dealt[:, a, :].rearrange("p (t mb mi b) -> p mb t mi b", t=PACK, mi=8, b=2),
-                wk_raw[:, a, :].rearrange("p (mb mi t b) -> p mb t mi b", t=PACK, mi=8, b=2),
-            )
+        wk_dealt = keep.tile([P, PASSES, N], U16, name="wk_dealt", align_bytes=64)
+        nc.vector.tensor_copy(
+            wk_dealt[:].rearrange("p a (t mb mi) -> p a mb t mi", t=PACK, mi=8),
+            wk_raw[:].rearrange("p a (mb mi t) -> p a mb t mi", t=PACK, mi=8),
+        )
         wv_dealt = [keep.tile([P, N], I32, name=f"wv_dealt{a}", align_bytes=64) for a in range(PASSES)]
         for a in range(PASSES):
             nc.vector.tensor_copy(
@@ -244,7 +243,7 @@ def tile_list_hwayreluP_kernel(
                 for s in range(0, width, P):
                     nc.tensor.matmul_mx(
                         banks[c][b][0][:, u * width + s : u * width + s + P],
-                        lhsT=wk_dealt[:, a, 2 * t * P : 2 * (t + 1) * P].bitcast(FP4X4),
+                        lhsT=wk_dealt[:, a, t * P : (t + 1) * P].bitcast(FP4X4),
                         lhsT_scale=scale_dealt[:, a, t * P : (t + 1) * P],
                         rhs=codes[:, j0 + s : j0 + s + P].bitcast(FP8X4),
                         rhs_scale=scales[:, j0 + s : j0 + s + P],

@@ -23,7 +23,6 @@ PASSES = K // (P * PACK)
 GROUP = 16
 QUADS = 4
 ROWS = 16
-WV_ROW = 4
 HALF = J // 2
 FIRST_CUTS = [slice(0, J // 4), slice(J // 4, HALF), slice(HALF, J)]
 HEADS = P // GROUP
@@ -71,41 +70,42 @@ def tile_list_hwayreluP_kernel(
         ]
         wgt_sb = keep.tile([P, J], F32, name="wgt_sb")
         wv_raw = [keep.tile([P, N], I32, name=f"wv_raw{a}") for a in range(PASSES)]
-        scale_raw = keep.tile([P, PASSES, N], U8, name="scale_raw")
+        scale_raw = keep.tile([P, 2, N], U8, name="scale_raw")
         for rows in (slice(32, 64), slice(64, P)):
             nc.gpsimd.memset(scale_raw[rows].bitcast(I32), 0)
         for s, scales in enumerate((wk_scales, wv_scales)):
             nc.sync.dma_start(
-                scale_raw[ROWS * s : ROWS * (s + 1)].bitcast(I32), scales.rearrange("a q n -> q a n").bitcast(I32)
+                scale_raw[0 : PASSES * ROWS, s, :].bitcast(I32), scales.rearrange("a q n -> (a q) n").bitcast(I32)
             )
-        scale_rows = keep.tile([P, PASSES, N], U8, name="scale_rows")
+        scale_rows = keep.tile([P, 2, N], U8, name="scale_rows")
         nc.vector.tensor_copy(
             scale_rows[:].rearrange("p a (t mb mi) -> p a mb t mi", t=PACK, mi=16),
             scale_raw[:].rearrange("p a (mb mi t) -> p a mb t mi", t=PACK, mi=16),
         )
-        scale_dealt = keep.tile([P, PASSES, N], U8, name="scale_dealt", align_bytes=64)
-        nc.gpsimd.memset(scale_dealt[:].bitcast(I32), 0)
+        scale_dealt = [keep.tile([P, 2, N], U8, name=f"scale_dealt{a}", align_bytes=64) for a in range(PASSES)]
+        for a in range(PASSES):
+            nc.gpsimd.memset(scale_dealt[a][:].bitcast(I32), 0)
         bias = keep.tile([P, PACK], F32, name="bias")
         neg_bias = keep.tile([P, PACK], F32, name="neg_bias")
         warm_out = keep.tile([P, 8], F32, name="warm_out")
         nc.scalar.activation(warm_out[HEADS * PIECES : P, :], wgt_rows[HEADS * PIECES : P, 0:8], ACT.Sigmoid)
 
-        def load_scales(q):
-            for s, row0 in enumerate((0, WV_ROW)):
+        def move_scales(a):
+            for q in range(QUADS):
                 nc.sync.dma_start(
-                    scale_dealt[32 * q + row0 : 32 * q + row0 + 4].bitcast(I32),
-                    scale_rows[ROWS * s + 4 * q : ROWS * s + 4 * q + 4].bitcast(I32),
+                    scale_dealt[a][32 * q : 32 * q + 4].bitcast(I32),
+                    scale_rows[ROWS * a + 4 * q : ROWS * a + 4 * q + 4].bitcast(I32),
                 )
 
         for i in range(PACK):
             nc.sync.dma_start(planes[0][i][:], x_rows[0, i])
-        for i in range(QUADS // 2):
-            load_scales(2 * i)
-            load_scales(2 * i + 1)
+        for i in range(2):
             nc.sync.dma_start(planes[1][i][:], x_rows[1, i])
         wv_rows = wv_words.rearrange("a p n i -> a p (n i)").bitcast(I32)
         nc.sync.dma_start(wv_raw[0][:], wv_rows[0])
+        move_scales(0)
         nc.sync.dma_start(planes[1][2][:], x_rows[1, 2])
+        move_scales(1)
         nc.sync.dma_start(planes[1][3][:], x_rows[1, 3])
         nc.sync.dma_start(wv_raw[1][:], wv_rows[1])
         nc.sync.dma_start(bias[:], bg.rearrange("(p t) -> p t", t=PACK))
@@ -244,7 +244,7 @@ def tile_list_hwayreluP_kernel(
                     nc.tensor.matmul_mx(
                         banks[c][b][0][:, u * width + s : u * width + s + P],
                         lhsT=wk_dealt[:, a, t * P : (t + 1) * P].bitcast(FP4X4),
-                        lhsT_scale=scale_dealt[:, a, t * P : (t + 1) * P],
+                        lhsT_scale=scale_dealt[a][:, 0, t * P : (t + 1) * P],
                         rhs=codes[:, j0 + s : j0 + s + P].bitcast(FP8X4),
                         rhs_scale=scales[:, j0 + s : j0 + s + P],
                         start=(a == 0 and u == 0 and s == 0),
@@ -260,7 +260,7 @@ def tile_list_hwayreluP_kernel(
                 nc.tensor.matmul_mx(
                     banks[c][b][1][:, u * width : (u + 1) * width],
                     lhsT=wv_dealt[a][:, t * P : (t + 1) * P].bitcast(FP8X4),
-                    lhsT_scale=scale_dealt[WV_ROW:P, a, t * P : (t + 1) * P],
+                    lhsT_scale=scale_dealt[a][:, 1, t * P : (t + 1) * P],
                     rhs=codes[:, j0 : j0 + width].bitcast(FP8X4),
                     rhs_scale=scales[:, j0 : j0 + width],
                     start=(a == 0 and u == 0),

@@ -161,7 +161,7 @@ def tile_list_hwayreluP_kernel(
             )
 
         picked0 = keep.tile([P, PACK, J], F32, name="picked0")
-        for cols in FIRST_CUTS:
+        for cols in (slice(0, HALF), slice(HALF, J)):
             gather(picked0[:, 0, cols], 0, 0, cols)
         for i in range(1, PACK):
             gather(picked0[:, i, :], 0, i, slice(0, J))
@@ -323,11 +323,14 @@ def tile_list_hwayreluP_kernel(
             if c >= EARLY:
                 open_banks(c)
                 multiply_k(c, 0)
-            multiply_k(c, 1)
+            if c != 1:
+                multiply_k(c, 1)
             for b in range(len(banks[c])):
                 if c >= EARLY:
                     multiply_v(c, 0, b)
                 multiply_v(c, 1, b)
+            if c == 1:
+                multiply_k(c, 1)
             read_banks(c)
 
         def product(engine, dst, c, span):

@@ -35,7 +35,7 @@ CHUNKS = len(WIDTHS)
 LAST = CHUNKS - 1
 EARLY = 2
 AHEAD = 2
-GPSIMD_FIRST = {128: 192, 256: 320}
+GPSIMD_FIRST = {128: 256, 256: 416}
 GPSIMD_LAST = {128: 384, 256: 512}
 
 

@@ -33,9 +33,10 @@ WIDTHS = [128, 256, 256, 256, 128]
 STARTS = [sum(WIDTHS[:c]) for c in range(len(WIDTHS))]
 CHUNKS = len(WIDTHS)
 LAST = CHUNKS - 1
+PARTS = [1, 1, 1, 2, 1]
 EARLY = 2
 AHEAD = 2
-GPSIMD_FIRST = {128: 256, 256: 416}
+GPSIMD_FIRST = [0, 128, 288, 288, 192]
 GPSIMD_LAST = {128: 384, 256: 512}
 
 
@@ -111,9 +112,18 @@ def tile_list_hwayreluP_kernel(
         nc.sync.dma_start(bias[:], bg.rearrange("(p t) -> p t", t=PACK))
         nc.scalar.mul(neg_bias[:], bias[:], -1.0)
         res_rows = res.rearrange("(p t) j -> p t j", t=PACK)
-        res_sb = [keep.tile([P, PACK, WIDTHS[c]], F32, name=f"res{c}") for c in range(CHUNKS)]
+
+        def values(c, name):
+            return keep.tile([P, PARTS[c], PACK, WIDTHS[c] // PARTS[c]], F32, name=f"{name}{c}")
+
+        def part(c, h):
+            width = WIDTHS[c] // PARTS[c]
+            return slice(STARTS[c] + h * width, STARTS[c] + (h + 1) * width)
+
+        res_sb = [values(c, "res") for c in range(CHUNKS)]
         for c in range(CHUNKS):
-            nc.sync.dma_start(res_sb[c][:], res_rows[:, :, chunk(c)])
+            for h in range(PARTS[c]):
+                nc.sync.dma_start(res_sb[c][:, h], res_rows[:, :, part(c, h)])
 
         turned = psum.tile([P, BANK], F32, name="turned", tag="sum")
         nc.tensor.transpose(turned[:, 0:P], wgt_rows[:], identity[:])
@@ -177,7 +187,7 @@ def tile_list_hwayreluP_kernel(
         nc.vector.quantize_mx(codes0[:].bitcast(FP8X4), scales0[:], woven0[:])
 
         def first_share(c):
-            return GPSIMD_FIRST[min(WIDTHS[c - 1], WIDTHS[c])] if c > 0 else 0
+            return GPSIMD_FIRST[c]
 
         def last_start(c):
             return PACK * WIDTHS[c] - (GPSIMD_LAST[min(WIDTHS[c], WIDTHS[c + 1])] if c < LAST else 0)
@@ -252,63 +262,65 @@ def tile_list_hwayreluP_kernel(
                     )
 
         def multiply_v(c, a, b):
-            width = WIDTHS[c]
+            width = WIDTHS[c] // PARTS[c]
             per_bank = BANK // width
             codes, scales, j0 = moving(c, a)
             for u in range(per_bank):
-                t = b * per_bank + u
+                h, t = divmod(b * per_bank + u, PACK)
+                cols = slice(j0 + h * width, j0 + (h + 1) * width)
                 nc.tensor.matmul_mx(
                     banks[c][b][1][:, u * width : (u + 1) * width],
                     lhsT=wv_dealt[a][:, t * P : (t + 1) * P].bitcast(FP8X4),
                     lhsT_scale=scale_dealt[a][:, 1, t * P : (t + 1) * P],
-                    rhs=codes[:, j0 : j0 + width].bitcast(FP8X4),
-                    rhs_scale=scales[:, j0 : j0 + width],
+                    rhs=codes[:, cols].bitcast(FP8X4),
+                    rhs_scale=scales[:, cols],
                     start=(a == 0 and u == 0),
                     stop=(a == PASSES - 1 and u == per_bank - 1),
                 )
 
+        def flat(tile):
+            return tile[:].rearrange("p h t j -> p (h t j)")
+
         def read_banks(c):
             width = WIDTHS[c]
             per_bank = BANK // width
-            gate[c] = keep.tile([P, PACK, width], F32, name=f"gate{c}")
-            diff[c] = keep.tile([P, PACK, width], F32, name=f"diff{c}")
+            gate[c] = values(c, "gate")
+            diff[c] = values(c, "diff")
             for b, (ke, ve) in enumerate(banks[c]):
                 for u in range(per_bank):
                     t = b * per_bank + u
-                    sums = ke[:, u * width : (u + 1) * width]
-                    nc.scalar.activation(gate[c][:, t, :], sums, ACT.Sigmoid, bias=neg_bias[:, t : t + 1], scale=-1.0)
-                rows = slice(b * per_bank, (b + 1) * per_bank)
+                    sums = ke[:, u * width : (u + 1) * width].rearrange("p (h j) -> p h j", h=PARTS[c])
+                    nc.scalar.activation(gate[c][:, :, t, :], sums, ACT.Sigmoid, bias=neg_bias[:, t : t + 1], scale=-1.0)
+                span = slice(b * BANK, (b + 1) * BANK)
                 nc.vector.scalar_tensor_tensor(
-                    diff[c][:, rows, :].rearrange("p t j -> p (t j)"),
-                    ve[:],
-                    0.0,
-                    res_sb[c][:, rows, :].rearrange("p t j -> p (t j)"),
-                    ALU.max,
-                    ALU.subtract,
+                    flat(diff[c])[:, span], ve[:], 0.0, flat(res_sb[c])[:, span], ALU.max, ALU.subtract
                 )
-
-        def flat(tile):
-            return tile[:].rearrange("p t j -> p (t j)")
 
         def weave_y(c, copy, cols):
             woven = woven_tile("y", c, cols.stop - cols.start, f"y_woven{c}_{cols.start}")
-            weave(copy, woven[:], y[c][:, :, cols])
+            weave(copy, woven[:], y[c][:, 0, :, cols])
             return woven
 
         def quantise_y(c, woven, cols):
-            y_codes = y_words[c][:, cols]
-            scales = y_scales[:, STARTS[c] + cols.start : STARTS[c] + cols.stop]
-            nc.vector.quantize_mx(y_codes.bitcast(FP8X4), scales, woven[:])
+            place = slice(STARTS[c] + cols.start, STARTS[c] + cols.stop)
+            nc.vector.quantize_mx(words(place).bitcast(FP8X4), y_scales[:, place], woven[:])
 
-        def store_words(c):
-            nc.sync.dma_start(out_words[:, chunk(c)], y_words[c][:].bitcast(I32))
+        def store_words(cols):
+            nc.sync.dma_start(out_words[:, cols], words(cols).bitcast(I32))
 
         def hand_on(c):
             whole = slice(0, WIDTHS[c])
             quantise_y(c, weave_y(c, nc.scalar.copy, whole), whole)
-            store_words(c)
 
-        y_words = [keep.tile([P, WIDTHS[c]], U32, name=f"y_words{c}", align_bytes=64) for c in range(CHUNKS)]
+        y_words = keep.tile([P, J], U32, name="y_words", align_bytes=64)
+        held = slice(STARTS[LAST - 2], STARTS[LAST - 1] + P)
+        held_words = {}
+
+        def words(cols):
+            if held.start <= cols.start < held.stop:
+                return held_words[0][:, cols.start - held.start : cols.stop - held.start]
+            return y_words[:, cols]
+
         for c in range(EARLY):
             open_banks(c)
             multiply_k(c, 0)
@@ -346,17 +358,23 @@ def tile_list_hwayreluP_kernel(
                 span = slice(max(lo, start), min(lo + BANK, stop))
                 finish(c, span, made[:, span.start - start : span.stop - start])
                 if span.stop % BANK == 0:
-                    rows = slice((span.stop - BANK) // WIDTHS[c], span.stop // WIDTHS[c])
-                    nc.sync.dma_start(out_rows[:, rows, chunk(c)], y[c][:, rows, :])
+                    width = WIDTHS[c] // PARTS[c]
+                    h, t = divmod((span.stop - BANK) // width, PACK)
+                    rows = slice(t, t + BANK // width)
+                    nc.sync.dma_start(out_rows[:, rows, part(c, h)], y[c][:, h, rows, :])
 
         late = {}
         for c in range(CHUNKS):
             sums(c)
-            y[c] = keep.tile([P, PACK, WIDTHS[c]], F32, name=f"y{c}")
+            y[c] = values(c, "y")
             step[c] = keep.tile([P, last_start(c)], F32, name=f"step{c}")
             if c >= 1:
                 finish_span(c - 1, 0, last_start(c - 1), step[c - 1][:])
-                product(nc.gpsimd, step[c][:, : first_share(c)], c, slice(0, first_share(c)))
+                if c == LAST:
+                    first_made = keep.tile([P, held.stop - held.start], F32, name="first_made", tag="held", align_bytes=64)
+                    product(nc.gpsimd, first_made[:, : first_share(c)], c, slice(0, first_share(c)))
+                else:
+                    product(nc.gpsimd, step[c][:, : first_share(c)], c, slice(0, first_share(c)))
                 finish_span(c - 1, last_start(c - 1), PACK * WIDTHS[c - 1], late[c - 1][:])
             if c + AHEAD + 2 < CHUNKS:
                 gather_last_plane(c + AHEAD + 2)
@@ -366,19 +384,26 @@ def tile_list_hwayreluP_kernel(
                         quantise_pass1(b)
                     else:
                         hand_on(b)
+                        store_words(chunk(b))
                 span = slice(last_start(c), PACK * WIDTHS[c])
                 late[c] = placed.tile([P, span.stop - span.start], F32, name=f"late{c}", offset=late_at[c], align_bytes=64)
                 product(nc.gpsimd, late[c][:], c, span)
             span = slice(first_share(c), last_start(c))
             product(nc.vector, step[c][:, span], c, span)
+        finish_span(LAST, 0, first_share(LAST), first_made[:, : first_share(LAST)])
+        held_words[0] = keep.tile([P, held.stop - held.start], U32, name="held_words", tag="held", align_bytes=64)
+        finish_span(LAST, first_share(LAST), last_start(LAST), step[LAST][:, first_share(LAST) :])
         hand_on(LAST - 2)
-        finish_span(LAST, 0, last_start(LAST), step[LAST][:])
-        hand_on(LAST - 1)
-        parts = [slice(0, WIDTHS[LAST] // 2), slice(WIDTHS[LAST] // 2, WIDTHS[LAST])]
-        woven_parts = [weave_y(LAST, copy, cols) for copy, cols in zip((nc.scalar.copy, nc.vector.tensor_copy), parts)]
-        for cols, woven in zip(parts, woven_parts):
-            quantise_y(LAST, woven, cols)
-        store_words(LAST)
+        half = WIDTHS[LAST] // 2
+        woven_first = weave_y(LAST - 1, nc.scalar.copy, slice(0, P))
+        woven_last = keep.tile([P, 2 * BANK], BF16, name="woven_last", align_bytes=64)
+        weave(nc.scalar.copy, woven_last[:, :BANK], y[LAST - 1][:, 1])
+        weave(nc.vector.tensor_copy, woven_last[:, BANK : BANK + PACK * half], y[LAST][:, 0, :, :half])
+        quantise_y(LAST - 1, woven_first, slice(0, P))
+        store_words(slice(STARTS[LAST - 2], STARTS[LAST - 1] + P))
+        weave(nc.scalar.copy, woven_last[:, BANK + PACK * half :], y[LAST][:, 0, :, half:])
+        quantise_y(LAST - 1, woven_last, slice(P, 3 * P))
+        store_words(slice(STARTS[LAST - 1] + P, J))
         for q in range(QUADS):
             queue = nc.scalar if q % 2 else nc.sync
             queue.dma_start(out_2[0, 4 * q : 4 * q + 4, :].bitcast(I32), y_scales[32 * q : 32 * q + 4, :].bitcast(I32))

@@ -36,7 +36,7 @@ LAST = CHUNKS - 1
 PARTS = [1, 1, 1, 2, 1]
 EARLY = 2
 AHEAD = 2
-GPSIMD_FIRST = [0, 128, 288, 288, 192]
+GPSIMD_FIRST = [0, 128, 352, 288, 256]
 GPSIMD_LAST = {128: 384, 256: 512}
 
 
@@ -394,7 +394,7 @@ def tile_list_hwayreluP_kernel(
         held_words[0] = keep.tile([P, held.stop - held.start], U32, name="held_words", tag="held", align_bytes=64)
         finish_span(LAST, first_share(LAST), last_start(LAST), step[LAST][:, first_share(LAST) :])
         hand_on(LAST - 2)
-        half = WIDTHS[LAST] // 2
+        half = 48
         woven_first = weave_y(LAST - 1, nc.scalar.copy, slice(0, P))
         woven_last = keep.tile([P, 2 * BANK], BF16, name="woven_last", align_bytes=64)
         weave(nc.scalar.copy, woven_last[:, :BANK], y[LAST - 1][:, 1])

from contextlib import ExitStack

import concourse.mybir as mybir
from concourse.masks import make_identity

K, N, T, J = 1024, 512, 2048, 1024
FLOPS = 2 * 2 * K * N * J

F32 = mybir.dt.float32
BF16 = mybir.dt.bfloat16
I32 = mybir.dt.int32
U32 = mybir.dt.uint32
U16 = mybir.dt.uint16
U8 = mybir.dt.uint8
FP8X4 = mybir.dt.float8_e4m3fn_x4
FP4X4 = mybir.dt.float4_e2m1fn_x4
ALU = mybir.AluOpType
ACT = mybir.ActivationFunctionType

P = 128
PACK = 4
PASSES = K // (P * PACK)
GROUP = 16
QUADS = 4
ROWS = 16
HALF = J // 2
FIRST_CUTS = [slice(0, J // 4), slice(J // 4, HALF), slice(HALF, J)]
HEADS = P // GROUP
PIECES = J // P
BANK = 512
BANKS = 8
WIDTHS = [128, 256, 256, 256, 128]
STARTS = [sum(WIDTHS[:c]) for c in range(len(WIDTHS))]
CHUNKS = len(WIDTHS)
LAST = CHUNKS - 1
PARTS = [1, 1, 1, 2, 1]
EARLY = 2
AHEAD = 2
GPSIMD_FIRST = [0, 128, 352, 288, 256]
GPSIMD_LAST = {128: 384, 256: 512}


def tile_list_hwayreluP_kernel(
    tc, xT, wgt, wk_words, wk_scales, wv_words, wv_scales, bg, res, offs, out_0, out_1, out_2
):
    nc = tc.nc
    with ExitStack() as ctx:
        keep = ctx.enter_context(tc.tile_pool(name="keep", bufs=1))
        psum = ctx.enter_context(tc.psum_pool(name="psum", bufs=BANKS))
        placed = ctx.enter_context(tc.tile_pool(name="placed", bufs=1))

        def chunk(c):
            return slice(STARTS[c], STARTS[c] + WIDTHS[c])

        wgt_rows = keep.tile([P, P], F32, name="wgt_rows")
        nc.vector.memset(wgt_rows[HEADS * PIECES : P, :], 0.0)
        nc.sync.dma_start(
            wgt_rows[0 : HEADS * PIECES, :], wgt.rearrange("(g s) (r c) -> s g r c", s=GROUP, r=PIECES)[0]
        )
        identity = keep.tile([P, P], F32, name="identity")
        make_identity(nc, identity[:])
        offsets = keep.tile([P, J // GROUP], U16, name="offsets")
        wk_raw = keep.tile([P, PASSES, N], U16, name="wk_raw")
        nc.sync.dma_start(wk_raw[:].bitcast(I32), wk_words.rearrange("a p b -> p a b").bitcast(I32))
        nc.sync.dma_start(offsets[:], offs)

        x_rows = xT.rearrange("(a p i) t -> a i p t", a=PASSES, i=PACK)
        planes = [
            [keep.tile([P, T], F32, name=f"x{a}{i}", tag=f"x{a}{i}", align_bytes=64) for i in range(PACK)]
            for a in range(PASSES)
        ]
        wgt_sb = keep.tile([P, J], F32, name="wgt_sb")
        wv_raw = [keep.tile([P, N], I32, name=f"wv_raw{a}") for a in range(PASSES)]
        scale_raw = keep.tile([P, 2, N], U8, name="scale_raw")
        for rows in (slice(32, 64), slice(64, P)):
            nc.gpsimd.memset(scale_raw[rows].bitcast(I32), 0)
        for s, scales in enumerate((wk_scales, wv_scales)):
            nc.sync.dma_start(
                scale_raw[0 : PASSES * ROWS, s, :].bitcast(I32), scales.rearrange("a q n -> (a q) n").bitcast(I32)
            )
        scale_rows = keep.tile([P, 2, N], U8, name="scale_rows")
        nc.vector.tensor_copy(
            scale_rows[:].rearrange("p a (t mb mi) -> p a mb t mi", t=PACK, mi=16),
            scale_raw[:].rearrange("p a (mb mi t) -> p a mb t mi", t=PACK, mi=16),
        )
        scale_dealt = [keep.tile([P, 2, N], U8, name=f"scale_dealt{a}", align_bytes=64) for a in range(PASSES)]
        for a in range(PASSES):
            nc.gpsimd.memset(scale_dealt[a][:].bitcast(I32), 0)
        bias = keep.tile([P, PACK], F32, name="bias")
        neg_bias = keep.tile([P, PACK], F32, name="neg_bias")
        warm_out = keep.tile([P, 8], F32, name="warm_out")
        nc.scalar.activation(warm_out[HEADS * PIECES : P, :], wgt_rows[HEADS * PIECES : P, 0:8], ACT.Sigmoid)

        def move_scales(a):
            for q in range(QUADS):
                nc.sync.dma_start(
                    scale_dealt[a][32 * q : 32 * q + 4].bitcast(I32),
                    scale_rows[ROWS * a + 4 * q : ROWS * a + 4 * q + 4].bitcast(I32),
                )

        for i in range(PACK):
            nc.sync.dma_start(planes[0][i][:], x_rows[0, i])
        for i in range(2):
            nc.sync.dma_start(planes[1][i][:], x_rows[1, i])
        wv_rows = wv_words.rearrange("a p n i -> a p (n i)").bitcast(I32)
        nc.sync.dma_start(wv_raw[0][:], wv_rows[0])
        move_scales(0)
        nc.sync.dma_start(planes[1][2][:], x_rows[1, 2])
        move_scales(1)
        nc.sync.dma_start(planes[1][3][:], x_rows[1, 3])
        nc.sync.dma_start(wv_raw[1][:], wv_rows[1])
        nc.sync.dma_start(bias[:], bg.rearrange("(p t) -> p t", t=PACK))
        nc.scalar.mul(neg_bias[:], bias[:], -1.0)
        res_rows = res.rearrange("(p t) j -> p t j", t=PACK)

        def values(c, name):
            return keep.tile([P, PARTS[c], PACK, WIDTHS[c] // PARTS[c]], F32, name=f"{name}{c}")

        def part(c, h):
            width = WIDTHS[c] // PARTS[c]
            return slice(STARTS[c] + h * width, STARTS[c] + (h + 1) * width)

        res_sb = [values(c, "res") for c in range(CHUNKS)]
        for c in range(CHUNKS):
            for h in range(PARTS[c]):
                nc.sync.dma_start(res_sb[c][:, h], res_rows[:, :, part(c, h)])

        turned = psum.tile([P, BANK], F32, name="turned", tag="sum")
        nc.tensor.transpose(turned[:, 0:P], wgt_rows[:], identity[:])
        by_piece = turned[:, 0 : HEADS * PIECES].rearrange("p (g r) -> p r g", r=PIECES)
        repeated = []
        for cols in FIRST_CUTS:
            count = (cols.stop - cols.start) // P
            wide = keep.tile([P, count, HEADS, GROUP], F32, name=f"repeated{cols.start}")
            source = by_piece[:, cols.start // P : cols.stop // P, :].unsqueeze(3)
            nc.scalar.copy(wide[:], source.to_broadcast([P, count, HEADS, GROUP]))
            repeated.append(wide)
        for cols, wide in zip(FIRST_CUTS, repeated):
            width = cols.stop - cols.start
            back = psum.tile([P, BANK], F32, name="back", tag="sum")
            for r in range(width // P):
                nc.tensor.transpose(back[:, r * P : (r + 1) * P], wide[:, r].rearrange("p g s -> p (g s)"), identity[:])
            nc.scalar.copy(wgt_sb[:, cols], back[:, 0:width])

        wk_dealt = keep.tile([P, PASSES, N], U16, name="wk_dealt", align_bytes=64)
        nc.vector.tensor_copy(
            wk_dealt[:].rearrange("p a (t mb mi) -> p a mb t mi", t=PACK, mi=8),
            wk_raw[:].rearrange("p a (mb mi t) -> p a mb t mi", t=PACK, mi=8),
        )
        wv_dealt = [keep.tile([P, N], I32, name=f"wv_dealt{a}", align_bytes=64) for a in range(PASSES)]
        for a in range(PASSES):
            nc.vector.tensor_copy(
                wv_dealt[a][:].rearrange("p (t mb mi) -> p mb t mi", t=PACK, mi=4),
                wv_raw[a][:].rearrange("p (mb mi t) -> p mb t mi", t=PACK, mi=4),
            )

        def gather(dst, a, i, cols):
            picks = offsets[:, cols.start // GROUP : cols.stop // GROUP]
            nc.vector.tensor_tensor(dst, planes[a][i][:].indirect(picks), wgt_sb[:, cols], ALU.mult)

        def weave(copy, dst, src):
            copy(
                dst.rearrange("p (c i t) -> p c t i", i=4, t=PACK),
                src.rearrange("p t (c i) -> p c t i", i=4),
            )

        def weave_pair(dst, src, u):
            nc.scalar.copy(
                dst.rearrange("p (c i t) -> p c t i", i=4, t=PACK)[:, :, 2 * u : 2 * u + 2, :],
                src.rearrange("p t (c i) -> p c t i", i=4),
            )

        picked0 = keep.tile([P, PACK, J], F32, name="picked0")
        for cols in (slice(0, HALF), slice(HALF, J)):
            gather(picked0[:, 0, cols], 0, 0, cols)
        for i in range(1, PACK):
            gather(picked0[:, i, :], 0, i, slice(0, J))
        woven0 = keep.tile([P, PACK * J], BF16, name="woven0", align_bytes=64)
        for u in range(2):
            weave_pair(woven0[:], picked0[:, 2 * u : 2 * u + 2, :], u)

        picked1 = keep.tile([P, PACK, J], F32, name="picked1")
        for i in range(2):
            gather(picked1[:, i, :], 1, i, slice(0, J))
        codes0 = keep.tile([P, J], U32, name="codes0", tag="x11", align_bytes=64)
        scales0 = keep.tile([P, J], U8, name="scales0", align_bytes=64)
        nc.vector.quantize_mx(codes0[:].bitcast(FP8X4), scales0[:], woven0[:])

        def first_share(c):
            return GPSIMD_FIRST[c]

        def last_start(c):
            return PACK * WIDTHS[c] - (GPSIMD_LAST[min(WIDTHS[c], WIDTHS[c + 1])] if c < LAST else 0)

        quantised = [[("xg", 2), ("xg", 3)], [("xg", 4)], [("y", 0)], [("y", 1)]]
        input_at, late_at = {}, {}
        free = late_end = 0
        for c, inputs in enumerate(quantised):
            free = max(free, late_end)
            for kind, b in inputs:
                input_at[kind, b] = free
                free = free + 2 * PACK * WIDTHS[b]
            late_at[c] = (late_end if c else input_at[inputs[-1]]) - 64
            late_end = late_at[c] + 4 * (PACK * WIDTHS[c] - last_start(c))

        def woven_tile(kind, c, width, name):
            if (kind, c) in input_at:
                return placed.tile([P, PACK * width], BF16, name=name, offset=input_at[kind, c], align_bytes=64)
            return keep.tile([P, PACK * width], BF16, name=name, align_bytes=64)

        woven1 = [woven_tile("xg", c, WIDTHS[c], f"woven1_{c}") for c in range(CHUNKS)]
        for c in range(CHUNKS):
            weave_pair(woven1[c][:], picked1[:, 0:2, chunk(c)], 0)
        gather(picked1[:, 2, :], 1, 2, slice(0, J))

        def gather_last_plane(c):
            gather(picked1[:, PACK - 1, chunk(c)], 1, PACK - 1, chunk(c))
            weave_pair(woven1[c][:], picked1[:, 2:PACK, chunk(c)], 1)

        out_rows = out_0.rearrange("(p t) j -> p t j", t=PACK)
        out_words = out_1[0].rearrange("p j i -> p (j i)").bitcast(I32)
        y_scales = keep.tile([P, J], U8, name="y_scales", align_bytes=64)
        operand1, banks, gate, diff, step, y = {}, {}, {}, {}, {}, {}

        def quantise_pass1(c):
            woven = woven1[c]
            codes = keep.tile([P, WIDTHS[c]], U32, name=f"codes1_{c}", align_bytes=64)
            scales = keep.tile([P, WIDTHS[c]], U8, name=f"scales1_{c}", align_bytes=64)
            nc.vector.quantize_mx(codes[:].bitcast(FP8X4), scales[:], woven[:])
            operand1[c] = (codes, scales)

        def open_banks(c):
            count = PACK * WIDTHS[c] // BANK
            if c == 2:
                ke = [psum.tile([P, BANK], F32, name="ke", tag="sum") for b in range(count)]
                ve = [psum.tile([P, BANK], F32, name="ve", tag="sum") for b in range(count)]
                banks[c] = list(zip(ke, ve))
            else:
                banks[c] = [
                    (psum.tile([P, BANK], F32, name="ke", tag="sum"), psum.tile([P, BANK], F32, name="ve", tag="sum"))
                    for b in range(count)
                ]

        def moving(c, a):
            return (codes0, scales0, STARTS[c]) if a == 0 else (operand1[c][0], operand1[c][1], 0)

        def multiply_k(c, a):
            width = WIDTHS[c]
            per_bank = BANK // width
            codes, scales, j0 = moving(c, a)
            for t in range(PACK):
                b, u = divmod(t, per_bank)
                for s in range(0, width, P):
                    nc.tensor.matmul_mx(
                        banks[c][b][0][:, u * width + s : u * width + s + P],
                        lhsT=wk_dealt[:, a, t * P : (t + 1) * P].bitcast(FP4X4),
                        lhsT_scale=scale_dealt[a][:, 0, t * P : (t + 1) * P],
                        rhs=codes[:, j0 + s : j0 + s + P].bitcast(FP8X4),
                        rhs_scale=scales[:, j0 + s : j0 + s + P],
                        start=(a == 0 and u == 0 and s == 0),
                        stop=(a == PASSES - 1 and u == per_bank - 1 and s == width - P),
                    )

        def multiply_v(c, a, b):
            width = WIDTHS[c] // PARTS[c]
            per_bank = BANK // width
            codes, scales, j0 = moving(c, a)
            for u in range(per_bank):
                h, t = divmod(b * per_bank + u, PACK)
                cols = slice(j0 + h * width, j0 + (h + 1) * width)
                nc.tensor.matmul_mx(
                    banks[c][b][1][:, u * width : (u + 1) * width],
                    lhsT=wv_dealt[a][:, t * P : (t + 1) * P].bitcast(FP8X4),
                    lhsT_scale=scale_dealt[a][:, 1, t * P : (t + 1) * P],
                    rhs=codes[:, cols].bitcast(FP8X4),
                    rhs_scale=scales[:, cols],
                    start=(a == 0 and u == 0),
                    stop=(a == PASSES - 1 and u == per_bank - 1),
                )

        def flat(tile):
            return tile[:].rearrange("p h t j -> p (h t j)")

        def read_banks(c):
            width = WIDTHS[c]
            per_bank = BANK // width
            gate[c] = values(c, "gate")
            diff[c] = values(c, "diff")
            for b, (ke, ve) in enumerate(banks[c]):
                for u in range(per_bank):
                    t = b * per_bank + u
                    sums = ke[:, u * width : (u + 1) * width].rearrange("p (h j) -> p h j", h=PARTS[c])
                    nc.scalar.activation(gate[c][:, :, t, :], sums, ACT.Sigmoid, bias=neg_bias[:, t : t + 1], scale=-1.0)
                span = slice(b * BANK, (b + 1) * BANK)
                nc.vector.scalar_tensor_tensor(
                    flat(diff[c])[:, span], ve[:], 0.0, flat(res_sb[c])[:, span], ALU.max, ALU.subtract
                )

        def weave_y(c, copy, cols):
            woven = woven_tile("y", c, cols.stop - cols.start, f"y_woven{c}_{cols.start}")
            weave(copy, woven[:], y[c][:, 0, :, cols])
            return woven

        def quantise_y(c, woven, cols):
            place = slice(STARTS[c] + cols.start, STARTS[c] + cols.stop)
            nc.vector.quantize_mx(words(place).bitcast(FP8X4), y_scales[:, place], woven[:])

        def store_words(cols):
            nc.sync.dma_start(out_words[:, cols], words(cols).bitcast(I32))

        def hand_on(c):
            whole = slice(0, WIDTHS[c])
            quantise_y(c, weave_y(c, nc.scalar.copy, whole), whole)

        y_words = keep.tile([P, J], U32, name="y_words", align_bytes=64)
        held = slice(STARTS[LAST - 2], STARTS[LAST - 1] + P)
        held_words = {}

        def words(cols):
            if held.start <= cols.start < held.stop:
                return held_words[0][:, cols.start - held.start : cols.stop - held.start]
            return y_words[:, cols]

        for c in range(EARLY):
            open_banks(c)
            multiply_k(c, 0)
            for b in range(len(banks[c])):
                multiply_v(c, 0, b)
        gather_last_plane(0)
        gather_last_plane(1)
        for c in range(AHEAD):
            quantise_pass1(c)
            gather_last_plane(c + 2)
        def sums(c):
            if c >= EARLY:
                open_banks(c)
                multiply_k(c, 0)
            if c != 1:
                multiply_k(c, 1)
            for b in range(len(banks[c])):
                if c >= EARLY:
                    multiply_v(c, 0, b)
                multiply_v(c, 1, b)
            if c == 1:
                multiply_k(c, 1)
            read_banks(c)

        def product(engine, dst, c, span):
            engine.tensor_tensor(dst, flat(diff[c])[:, span], flat(gate[c])[:, span], ALU.mult)

        def finish(c, span, made):
            b = span.start // BANK
            ve = banks[c][b][1][:, span.start - b * BANK : span.stop - b * BANK]
            nc.vector.scalar_tensor_tensor(flat(y[c])[:, span], ve, 0.0, made, ALU.max, ALU.subtract)

        def finish_span(c, start, stop, made):
            for lo in range(start - start % BANK, stop, BANK):
                span = slice(max(lo, start), min(lo + BANK, stop))
                finish(c, span, made[:, span.start - start : span.stop - start])
                if span.stop % BANK == 0:
                    width = WIDTHS[c] // PARTS[c]
                    h, t = divmod((span.stop - BANK) // width, PACK)
                    rows = slice(t, t + BANK // width)
                    nc.sync.dma_start(out_rows[:, rows, part(c, h)], y[c][:, h, rows, :])

        late = {}
        for c in range(CHUNKS):
            sums(c)
            y[c] = values(c, "y")
            step[c] = keep.tile([P, last_start(c)], F32, name=f"step{c}")
            if c >= 1:
                finish_span(c - 1, 0, last_start(c - 1), step[c - 1][:])
                if c == LAST:
                    first_made = keep.tile([P, held.stop - held.start], F32, name="first_made", tag="held", align_bytes=64)
                    product(nc.gpsimd, first_made[:, : first_share(c)], c, slice(0, first_share(c)))
                else:
                    product(nc.gpsimd, step[c][:, : first_share(c)], c, slice(0, first_share(c)))
                finish_span(c - 1, last_start(c - 1), PACK * WIDTHS[c - 1], late[c - 1][:])
            if c + AHEAD + 2 < CHUNKS:
                gather_last_plane(c + AHEAD + 2)
            if c < LAST:
                for kind, b in quantised[c]:
                    if kind == "xg":
                        quantise_pass1(b)
                    else:
                        hand_on(b)
                        store_words(chunk(b))
                span = slice(last_start(c), PACK * WIDTHS[c])
                late[c] = placed.tile([P, span.stop - span.start], F32, name=f"late{c}", offset=late_at[c], align_bytes=64)
                product(nc.gpsimd, late[c][:], c, span)
            span = slice(first_share(c), last_start(c))
            product(nc.vector, step[c][:, span], c, span)
        finish_span(LAST, 0, first_share(LAST), first_made[:, : first_share(LAST)])
        held_words[0] = keep.tile([P, held.stop - held.start], U32, name="held_words", tag="held", align_bytes=64)
        finish_span(LAST, first_share(LAST), last_start(LAST), step[LAST][:, first_share(LAST) :])
        hand_on(LAST - 2)
        half = 48
        woven_first = weave_y(LAST - 1, nc.scalar.copy, slice(0, P))
        woven_last = keep.tile([P, 2 * BANK], BF16, name="woven_last", align_bytes=64)
        weave(nc.scalar.copy, woven_last[:, :BANK], y[LAST - 1][:, 1])
        weave(nc.vector.tensor_copy, woven_last[:, BANK : BANK + PACK * half], y[LAST][:, 0, :, :half])
        quantise_y(LAST - 1, woven_first, slice(0, P))
        store_words(slice(STARTS[LAST - 2], STARTS[LAST - 1] + P))
        weave(nc.scalar.copy, woven_last[:, BANK + PACK * half :], y[LAST][:, 0, :, half:])
        quantise_y(LAST - 1, woven_last, slice(P, 3 * P))
        store_words(slice(STARTS[LAST - 1] + P, J))
        for q in range(QUADS):
            queue = nc.scalar if q % 2 else nc.sync
            queue.dma_start(out_2[0, 4 * q : 4 * q + 4, :].bitcast(I32), y_scales[32 * q : 32 * q + 4, :].bitcast(I32))
